import numpy as np
import ml_dtypes


def mxq(x, axis, fmt="e4m3"):
    dtype, down = {"e4m3": (ml_dtypes.float8_e4m3fn, 7), "e5m2": (ml_dtypes.float8_e5m2, 14)}[fmt]
    v = np.moveaxis(np.asarray(x, np.float32).astype(ml_dtypes.bfloat16).astype(np.float64), axis, -1)
    blocks = v.reshape(v.shape[:-1] + (-1, 32))
    amax = np.abs(blocks).max(-1, keepdims=True)
    byte = np.maximum(np.where(amax > 0, np.frexp(amax)[1] - 1 + 127, 0) - down, 1)
    scale = np.exp2(byte - 127.0)
    codes = (blocks / scale).astype(np.float32).astype(dtype).astype(np.float64)
    return np.moveaxis((codes * scale).reshape(v.shape), -1, axis)


WIDE = False


def mx_kscale(k):
    if not WIDE:
        return np.ones(k)
    levels = np.array([10, -10, 5, -5, 0])
    if k % 512:
        return np.exp2(np.random.permutation(np.resize(levels, k // 32))).repeat(32)
    a = np.empty((k // 512, 16))
    for p in range(k // 512):
        a[p, :8] = np.random.permutation(np.resize(levels, 8))
        for g in range(8):
            far = levels[np.abs(levels - a[p, g]) >= 10]
            a[p, g + 8] = far[np.random.randint(len(far))]
    return np.exp2(a.ravel()).repeat(32)


def f64(x):
    return np.asarray(x).astype(np.float64)


def striped(idx):
    return np.tile(idx.reshape(-1, 16).T, (8, 1)).astype(np.uint16)


def unstriped(offs):
    return offs[:16].T.reshape(-1).astype(np.int64)


def pack_weight(w):
    k, n = w.shape
    w = f64(np.asarray(w, np.float32).astype(ml_dtypes.bfloat16)).reshape(k // 32, 32, n)
    amax = np.abs(w).max(1)
    byte = np.clip(np.where(amax > 0, np.frexp(amax)[1] - 1 + 127 - 7, 1), 1, 254)
    scaled = (w * np.exp2(127.0 - byte)[:, None, :]).reshape(k, n).astype(np.float32)
    words = np.ascontiguousarray(scaled.reshape(k // 512, 128, 4, n).transpose(0, 1, 3, 2)).astype(ml_dtypes.float8_e4m3fn).view(np.uint8)
    return words, np.ascontiguousarray(byte.astype(np.uint8).reshape(k // 512, 16, n))


def unpack_weight(words, scales):
    g, p, n, _ = words.shape
    vals = np.ascontiguousarray(words).view(ml_dtypes.float8_e4m3fn).astype(np.float64) * np.repeat(np.exp2(scales.astype(np.float64) - 127.0), 8, axis=1)[..., None]
    return vals.transpose(0, 1, 3, 2).reshape(g * 512, n)


def silu(v):
    return v / (1.0 + np.exp(-np.maximum(v, -700.0)))


K, T, S, D, H, N = 512, 2048, 1024, 3, 512, 256


def setup_inputs():
    n = np.random.standard_normal
    s = mx_kscale(K)[:, None]
    u = mx_kscale(H)
    packed_xT = pack_weight(n((K, T)) * s)
    return {
        "x_words": packed_xT[0],
        "x_scales": packed_xT[1],
        "w1": (n((K, H)) / np.sqrt(K) / s * u).astype(np.float32),
        "w2": (n((H, N)) / np.sqrt(H) / u[:, None]).astype(np.float32),
        "taps": (n((H, D)) / np.sqrt(D)).astype(np.float32),
        "offs": striped(np.random.permutation(T)[:S]),
    }


def reference(x_words, x_scales, w1, w2, taps, offs):
    xq = unpack_weight(x_words, x_scales)[:, unstriped(offs)]
    h = mxq(f64(w1), 0, "e4m3").T @ xq
    z = silu(f64(taps)[:, 0:1] * h + f64(taps)[:, 1:2] * (np.pad(h, ((0, 0), (1, 0)))[:, :S]) + f64(taps)[:, 2:3] * (np.pad(h, ((0, 0), (2, 0)))[:, :S]))
    return mxq(f64(w2), 0, "e4m3").T @ mxq(z, 0, "e4m3")

@@ -1,0 +1,174 @@
+from contextlib import ExitStack
+
+import concourse.mybir as mybir
+
+K, T, S, D, H, N = 512, 2048, 1024, 3, 512, 256
+FLOPS = 2 * K * H * S + 2 * H * N * S
+
+F32 = mybir.dt.float32
+BF16 = mybir.dt.bfloat16
+I32 = mybir.dt.int32
+U32 = mybir.dt.uint32
+U16 = mybir.dt.uint16
+U8 = mybir.dt.uint8
+FP8X4 = mybir.dt.float8_e4m3fn_x4
+ACT = mybir.ActivationFunctionType
+MULT = mybir.AluOpType.mult
+ADD = mybir.AluOpType.add
+
+P = 128
+PACK = 4
+HALO = D - 1
+CHUNKS = (128, 256, 256, 256, 128)
+
+
+def tile_picked_dconv_silu_p_kernel(tc, x_words, x_scales, w1, w2, taps, offs, out):
+    nc = tc.nc
+    with ExitStack() as ctx:
+        keep = ctx.enter_context(tc.tile_pool(name="keep", bufs=1))
+        ring = ctx.enter_context(tc.tile_pool(name="ring", bufs=2))
+        psum_h = ctx.enter_context(tc.psum_pool(name="psum_h", bufs=6))
+        psum_o = ctx.enter_context(tc.psum_pool(name="psum_o", bufs=2))
+
+        offsets = keep.tile([P, S // 16], U16, name="offsets")
+        nc.sync.dma_start(offsets[:], offs)
+
+        all_scales = keep.tile([P, T], U8, name="all_scales", tag="scales_then_codes", align_bytes=64)
+        nc.vector.memset(all_scales[:].bitcast(I32), 0)
+        for q in range(4):
+            nc.scalar.dma_start(all_scales[32 * q : 32 * q + 4, :].bitcast(I32), x_scales[0, 4 * q : 4 * q + 4, :].bitcast(I32))
+
+        all_words = keep.tile([P, T], I32, name="all_words", align_bytes=64)
+        nc.sync.dma_start(all_words[:], x_words[0].rearrange("p n t -> p (n t)").bitcast(I32))
+
+        w1_rows = w1.rearrange("(p j) c -> p j c", j=PACK)
+        w1_raw = []
+        for half in range(2):
+            raw = keep.tile([P, PACK, H // 2], F32, name=f"w1_raw{half}")
+            nc.sync.dma_start(raw[:], w1_rows[:, :, half * (H // 2) : (half + 1) * (H // 2)])
+            w1_raw.append(raw)
+        w2_raw = keep.tile([P, PACK, N], F32, name="w2_raw")
+        nc.sync.dma_start(w2_raw[:], w2.rearrange("(p j) c -> p j c", j=PACK))
+        tap = keep.tile([P, PACK * D], F32, name="tap")
+        nc.gpsimd.dma_start(tap[:], taps.rearrange("(p t) d -> p (t d)", t=PACK))
+
+        zero = keep.tile([P, HALO], F32, name="zero")
+        nc.vector.memset(zero[:], 0.0)
+        acc = []
+        for t in range(PACK):
+            a = keep.tile([P, S + HALO], F32, name=f"acc{t}")
+            nc.scalar.activation(a[:, 0:HALO], zero[:], ACT.Silu)
+            acc.append(a)
+
+        x_scale = keep.tile([P, S], U8, name="x_scale", align_bytes=64)
+        nc.vector.tensor_copy(x_scale[:], all_scales[:].indirect(offsets[:]))
+        x_code = keep.tile([P, S], U32, name="x_code", tag="scales_then_codes", align_bytes=64)
+        nc.vector.tensor_copy(x_code[:], all_words[:].bitcast(U32).indirect(offsets[:]))
+
+        w1_bf = keep.tile([P, PACK * H], BF16, name="w1_bf", tag="w_bf", align_bytes=64)
+        w1_dst = w1_bf[:].rearrange("p (t m j) -> p m j t", t=PACK, j=PACK)
+        w1_src = [raw[:].rearrange("p j (m t) -> p m j t", t=PACK) for raw in w1_raw]
+        nc.scalar.copy(w1_dst[:, 0:64], w1_src[0])
+        nc.scalar.copy(w1_dst[:, 64:88], w1_src[1][:, 0:24])
+        nc.vector.tensor_copy(w1_dst[:, 88:128], w1_src[1][:, 24:64])
+        w1_code = keep.tile([P, H], U32, name="w1_code", align_bytes=64)
+        w1_scale = keep.tile([P, H], U8, name="w1_scale", align_bytes=64)
+        for t in range(PACK):
+            cols = slice(t * P, (t + 1) * P)
+            nc.vector.quantize_mx(
+                out=w1_code[:, cols].bitcast(FP8X4),
+                scales=w1_scale[:, cols],
+                in_=w1_bf[:, t * P * PACK : (t + 1) * P * PACK],
+            )
+
+        w2_bf = keep.tile([P, PACK * N], BF16, name="w2_bf", tag="w_bf", align_bytes=64)
+        w2_code = keep.tile([P, N], U32, name="w2_code", align_bytes=64)
+        w2_scale = keep.tile([P, N], U8, name="w2_scale", align_bytes=64)
+
+        def prepare_w2():
+            nc.gpsimd.tensor_scalar(
+                w2_bf[:].rearrange("p (c j) -> p c j", j=PACK),
+                w2_raw[:].rearrange("p j c -> p c j"),
+                1.0, 0.0, MULT, ADD,
+            )
+            nc.vector.quantize_mx(out=w2_code[:].bitcast(FP8X4), scales=w2_scale[:], in_=w2_bf[:])
+
+        out_rows = out.rearrange("(h p) s -> p h s", p=P)
+
+        def convolve_pair(j0, n, pair, conv):
+            banks = {}
+            for t in pair:
+                h = psum_h.tile([P, n], F32, name="h", tag="h")
+                cols = slice(t * P, (t + 1) * P)
+                nc.tensor.matmul_mx(
+                    out=h[:],
+                    lhsT=w1_code[:, cols].bitcast(FP8X4),
+                    lhsT_scale=w1_scale[:, cols],
+                    rhs=x_code[:, j0 : j0 + n].bitcast(FP8X4),
+                    rhs_scale=x_scale[:, j0 : j0 + n],
+                    start=True,
+                    stop=True,
+                )
+                nc.scalar.activation(acc[t][:, j0 + 2 : j0 + n + 2], h[:], ACT.Copy, scale=tap[:, D * t + 2 : D * t + 3])
+                banks[t] = h
+            for t in pair:
+                part = acc[t][:, j0 + 1 : j0 + n + 1]
+                nc.vector.scalar_tensor_tensor(part, banks[t][:], tap[:, D * t + 1 : D * t + 2], part, MULT, ADD)
+            for t in pair:
+                nc.vector.scalar_tensor_tensor(conv[:, t, :], banks[t][:], tap[:, D * t : D * t + 1], acc[t][:, j0 : j0 + n], MULT, ADD)
+
+        def activate_and_quantise(n, conv):
+            z = ring.tile([P, n * PACK], BF16, name="z", tag="z", align_bytes=64)
+            nc.scalar.activation(
+                z[:].rearrange("p (c i t) -> p c t i", i=4, t=PACK),
+                conv[:].rearrange("p t (c i) -> p c t i", i=4),
+                ACT.Silu,
+            )
+            z_code = ring.tile([P, n], U32, name="z_code", tag="z_code", align_bytes=64)
+            z_scale = ring.tile([P, n], U8, name="z_scale", tag="z_scale", align_bytes=64)
+            nc.vector.quantize_mx(out=z_code[:].bitcast(FP8X4), scales=z_scale[:], in_=z[:])
+            return z_code, z_scale
+
+        def second_product(dst, half, z_code, z_scale):
+            cols = slice(half * P, (half + 1) * P)
+            nc.tensor.matmul_mx(
+                out=dst,
+                lhsT=w2_code[:, cols].bitcast(FP8X4),
+                lhsT_scale=w2_scale[:, cols],
+                rhs=z_code[:].bitcast(FP8X4),
+                rhs_scale=z_scale[:],
+                start=True,
+                stop=True,
+            )
+
+        def project_and_store(j0, n, z_code, z_scale, copy):
+            o = psum_o.tile([P, 2, n], F32, name="o", tag="o")
+            for half in range(2):
+                second_product(o[:, half, :], half, z_code, z_scale)
+            res = keep.tile([P, 2, n], F32, name=f"res{j0}")
+            copy(res[:], o[:])
+            nc.sync.dma_start(out_rows[:, :, j0 : j0 + n], res[:])
+
+        starts = [sum(CHUNKS[:c]) for c in range(len(CHUNKS))]
+        previous = None
+        for c, (j0, n) in enumerate(zip(starts, CHUNKS)):
+            conv = ring.tile([P, PACK, n], F32, name="conv", tag="conv")
+            convolve_pair(j0, n, (0, 1), conv)
+            if previous is None:
+                prepare_w2()
+            else:
+                quantised = activate_and_quantise(previous[1], previous[2])
+            convolve_pair(j0, n, (2, 3), conv)
+            if previous is not None:
+                copy = nc.vector.tensor_copy if c == len(CHUNKS) - 1 else nc.scalar.copy
+                project_and_store(previous[0], previous[1], *quantised, copy)
+            previous = (j0, n, conv)
+
+        j0, n, conv = previous
+        z_code, z_scale = activate_and_quantise(n, conv)
+        for half, copy in enumerate((nc.scalar.copy, nc.vector.tensor_copy)):
+            o = psum_o.tile([P, n], F32, name="o_last", tag="o")
+            second_product(o[:], half, z_code, z_scale)
+            res = keep.tile([P, n], F32, name=f"res_last{half}")
+            copy(res[:], o[:])
+            nc.sync.dma_start(out_rows[:, half, j0 : j0 + n], res[:])

@@ -19,7 +19,12 @@ ADD = mybir.AluOpType.add
 P = 128
 PACK = 4
 HALO = D - 1
-CHUNKS = (128, 256, 256, 256, 128)
+CHUNKS = ((128,), (256, 128), (256, 128), (128,))
+VECTOR_COPIES = (512, 768)
+
+
+def spans(widths):
+    return [(sum(widths[:c]), width) for c, width in enumerate(widths)]
 
 
 def tile_picked_dconv_silu_p_kernel(tc, x_words, x_scales, w1, w2, taps, offs, out):
@@ -34,11 +39,13 @@ def tile_picked_dconv_silu_p_kernel(tc, x_words, x_scales, w1, w2, taps, offs, o
         nc.sync.dma_start(offsets[:], offs)
 
         all_scales = keep.tile([P, T], U8, name="all_scales", tag="scales_then_codes", align_bytes=64)
-        nc.vector.memset(all_scales[:].bitcast(I32), 0)
+        nc.gpsimd.memset(all_scales[:].bitcast(I32), 0)
+        tap = keep.tile([P, PACK * D], F32, name="tap")
+        nc.sync.dma_start(tap[:], taps.rearrange("(p t) d -> p (t d)", t=PACK))
         for q in range(4):
-            nc.scalar.dma_start(all_scales[32 * q : 32 * q + 4, :].bitcast(I32), x_scales[0, 4 * q : 4 * q + 4, :].bitcast(I32))
+            nc.sync.dma_start(all_scales[32 * q : 32 * q + 4, :].bitcast(I32), x_scales[0, 4 * q : 4 * q + 4, :].bitcast(I32))
 
-        all_words = keep.tile([P, T], I32, name="all_words", align_bytes=64)
+        all_words = keep.tile([P, T], I32, name="all_words", tag="words_then_w2", align_bytes=64)
         nc.sync.dma_start(all_words[:], x_words[0].rearrange("p n t -> p (n t)").bitcast(I32))
 
         w1_rows = w1.rearrange("(p j) c -> p j c", j=PACK)
@@ -49,8 +56,6 @@ def tile_picked_dconv_silu_p_kernel(tc, x_words, x_scales, w1, w2, taps, offs, o
             w1_raw.append(raw)
         w2_raw = keep.tile([P, PACK, N], F32, name="w2_raw")
         nc.sync.dma_start(w2_raw[:], w2.rearrange("(p j) c -> p j c", j=PACK))
-        tap = keep.tile([P, PACK * D], F32, name="tap")
-        nc.gpsimd.dma_start(tap[:], taps.rearrange("(p t) d -> p (t d)", t=PACK))
 
         zero = keep.tile([P, HALO], F32, name="zero")
         nc.vector.memset(zero[:], 0.0)
@@ -62,15 +67,22 @@ def tile_picked_dconv_silu_p_kernel(tc, x_words, x_scales, w1, w2, taps, offs, o
 
         x_scale = keep.tile([P, S], U8, name="x_scale", align_bytes=64)
         nc.vector.tensor_copy(x_scale[:], all_scales[:].indirect(offsets[:]))
-        x_code = keep.tile([P, S], U32, name="x_code", tag="scales_then_codes", align_bytes=64)
-        nc.vector.tensor_copy(x_code[:], all_words[:].bitcast(U32).indirect(offsets[:]))
+        x_code = []
+
+        def gather_words(half, tag):
+            code = keep.tile([P, S // 2], U32, name=f"x_code{half}", tag=tag, align_bytes=64)
+            entries = offsets[:, half * S // 32 : (half + 1) * S // 32]
+            nc.vector.tensor_copy(code[:], all_words[:].bitcast(U32).indirect(entries))
+            x_code.append(code)
+
+        gather_words(0, "scales_then_codes")
 
         w1_bf = keep.tile([P, PACK * H], BF16, name="w1_bf", tag="w_bf", align_bytes=64)
         w1_dst = w1_bf[:].rearrange("p (t m j) -> p m j t", t=PACK, j=PACK)
         w1_src = [raw[:].rearrange("p j (m t) -> p m j t", t=PACK) for raw in w1_raw]
         nc.scalar.copy(w1_dst[:, 0:64], w1_src[0])
-        nc.scalar.copy(w1_dst[:, 64:88], w1_src[1][:, 0:24])
-        nc.vector.tensor_copy(w1_dst[:, 88:128], w1_src[1][:, 24:64])
+        nc.scalar.copy(w1_dst[:, 64:80], w1_src[1][:, 0:16])
+        nc.vector.tensor_copy(w1_dst[:, 80:128], w1_src[1][:, 16:64])
         w1_code = keep.tile([P, H], U32, name="w1_code", align_bytes=64)
         w1_scale = keep.tile([P, H], U8, name="w1_scale", align_bytes=64)
         for t in range(PACK):
@@ -81,7 +93,9 @@ def tile_picked_dconv_silu_p_kernel(tc, x_words, x_scales, w1, w2, taps, offs, o
                 in_=w1_bf[:, t * P * PACK : (t + 1) * P * PACK],
             )
 
-        w2_bf = keep.tile([P, PACK * N], BF16, name="w2_bf", tag="w_bf", align_bytes=64)
+        gather_words(1, "w_bf")
+
+        w2_bf = keep.tile([P, PACK * N], BF16, name="w2_bf", tag="words_then_w2", align_bytes=64)
         w2_code = keep.tile([P, N], U32, name="w2_code", align_bytes=64)
         w2_scale = keep.tile([P, N], U8, name="w2_scale", align_bytes=64)
 
@@ -95,20 +109,22 @@ def tile_picked_dconv_silu_p_kernel(tc, x_words, x_scales, w1, w2, taps, offs, o
 
         out_rows = out.rearrange("(h p) s -> p h s", p=P)
 
-        def convolve_pair(j0, n, pair, conv):
+        def convolve_pair(j0, parts, pair, conv):
+            n = sum(parts)
             banks = {}
             for t in pair:
                 h = psum_h.tile([P, n], F32, name="h", tag="h")
                 cols = slice(t * P, (t + 1) * P)
-                nc.tensor.matmul_mx(
-                    out=h[:],
-                    lhsT=w1_code[:, cols].bitcast(FP8X4),
-                    lhsT_scale=w1_scale[:, cols],
-                    rhs=x_code[:, j0 : j0 + n].bitcast(FP8X4),
-                    rhs_scale=x_scale[:, j0 : j0 + n],
-                    start=True,
-                    stop=True,
-                )
+                for a, width in spans(parts):
+                    nc.tensor.matmul_mx(
+                        out=h[:, a : a + width],
+                        lhsT=w1_code[:, cols].bitcast(FP8X4),
+                        lhsT_scale=w1_scale[:, cols],
+                        rhs=x_code[j0 // (S // 2)][:, j0 % (S // 2) + a : j0 % (S // 2) + a + width].bitcast(FP8X4),
+                        rhs_scale=x_scale[:, j0 + a : j0 + a + width],
+                        start=True,
+                        stop=True,
+                    )
                 nc.scalar.activation(acc[t][:, j0 + 2 : j0 + n + 2], h[:], ACT.Copy, scale=tap[:, D * t + 2 : D * t + 3])
                 banks[t] = h
             for t in pair:
@@ -121,7 +137,7 @@ def tile_picked_dconv_silu_p_kernel(tc, x_words, x_scales, w1, w2, taps, offs, o
             z = ring.tile([P, n * PACK], BF16, name="z", tag="z", align_bytes=64)
             nc.scalar.activation(
                 z[:].rearrange("p (c i t) -> p c t i", i=4, t=PACK),
-                conv[:].rearrange("p t (c i) -> p c t i", i=4),
+                conv.rearrange("p t (c i) -> p c t i", i=4),
                 ACT.Silu,
             )
             z_code = ring.tile([P, n], U32, name="z_code", tag="z_code", align_bytes=64)
@@ -149,26 +165,30 @@ def tile_picked_dconv_silu_p_kernel(tc, x_words, x_scales, w1, w2, taps, offs, o
             copy(res[:], o[:])
             nc.sync.dma_start(out_rows[:, :, j0 : j0 + n], res[:])
 
-        starts = [sum(CHUNKS[:c]) for c in range(len(CHUNKS))]
-        previous = None
-        for c, (j0, n) in enumerate(zip(starts, CHUNKS)):
-            conv = ring.tile([P, PACK, n], F32, name="conv", tag="conv")
-            convolve_pair(j0, n, (0, 1), conv)
-            if previous is None:
-                prepare_w2()
+        def finish(j0, n, conv):
+            z_code, z_scale = activate_and_quantise(n, conv)
+            if j0 + n < S:
+                copy = nc.vector.tensor_copy if j0 in VECTOR_COPIES else nc.scalar.copy
+                project_and_store(j0, n, z_code, z_scale, copy)
             else:
-                quantised = activate_and_quantise(previous[1], previous[2])
-            convolve_pair(j0, n, (2, 3), conv)
-            if previous is not None:
-                copy = nc.vector.tensor_copy if c == len(CHUNKS) - 1 else nc.scalar.copy
-                project_and_store(previous[0], previous[1], *quantised, copy)
-            previous = (j0, n, conv)
+                for half, copy, queue in ((0, nc.scalar.copy, nc.scalar), (1, nc.vector.tensor_copy, nc.sync)):
+                    o = psum_o.tile([P, n], F32, name="o_last", tag="o")
+                    second_product(o[:], half, z_code, z_scale)
+                    res = keep.tile([P, n], F32, name=f"res_last{half}")
+                    copy(res[:], o[:])
+                    queue.dma_start(out_rows[:, half, j0 : j0 + n], res[:])
 
-        j0, n, conv = previous
-        z_code, z_scale = activate_and_quantise(n, conv)
-        for half, copy in enumerate((nc.scalar.copy, nc.vector.tensor_copy)):
-            o = psum_o.tile([P, n], F32, name="o_last", tag="o")
-            second_product(o[:], half, z_code, z_scale)
-            res = keep.tile([P, n], F32, name=f"res_last{half}")
-            copy(res[:], o[:])
-            nc.sync.dma_start(out_rows[:, half, j0 : j0 + n], res[:])
+        pending = []
+        for parts, (j0, n) in zip(CHUNKS, spans([sum(parts) for parts in CHUNKS])):
+            conv = ring.tile([P, PACK, n], F32, name="conv", tag="conv")
+            convolve_pair(j0, parts, (0, 1), conv)
+            if j0 == 0:
+                prepare_w2()
+            for args in pending[:1]:
+                finish(*args)
+            convolve_pair(j0, parts, (2, 3), conv)
+            for args in pending[1:]:
+                finish(*args)
+            pending = [(j0 + a, width, conv[:, :, a : a + width]) for a, width in spans(parts)]
+        for args in pending:
+            finish(*args)

@@ -19,8 +19,9 @@ ADD = mybir.AluOpType.add
 P = 128
 PACK = 4
 HALO = D - 1
+EARLY = 384
 CHUNKS = ((128,), (256, 128), (256, 128), (128,))
-VECTOR_COPIES = (512, 768)
+VECTOR_COPIES = (768,)
 
 
 def spans(widths):
@@ -31,29 +32,24 @@ def tile_picked_dconv_silu_p_kernel(tc, x_words, x_scales, w1, w2, taps, offs, o
     nc = tc.nc
     with ExitStack() as ctx:
         keep = ctx.enter_context(tc.tile_pool(name="keep", bufs=1))
-        ring = ctx.enter_context(tc.tile_pool(name="ring", bufs=2))
+        ring = ctx.enter_context(tc.tile_pool(name="ring", bufs=3))
         psum_h = ctx.enter_context(tc.psum_pool(name="psum_h", bufs=6))
         psum_o = ctx.enter_context(tc.psum_pool(name="psum_o", bufs=2))
 
         offsets = keep.tile([P, S // 16], U16, name="offsets")
         nc.sync.dma_start(offsets[:], offs)
 
-        all_scales = keep.tile([P, T], U8, name="all_scales", tag="scales_then_codes", align_bytes=64)
+        all_scales = keep.tile([P, T], U8, name="all_scales", align_bytes=64)
         nc.gpsimd.memset(all_scales[:].bitcast(I32), 0)
         tap = keep.tile([P, PACK * D], F32, name="tap")
         nc.sync.dma_start(tap[:], taps.rearrange("(p t) d -> p (t d)", t=PACK))
         for q in range(4):
             nc.sync.dma_start(all_scales[32 * q : 32 * q + 4, :].bitcast(I32), x_scales[0, 4 * q : 4 * q + 4, :].bitcast(I32))
 
+        w1_raw = keep.tile([P, PACK, H], F32, name="w1_raw")
+        nc.sync.dma_start(w1_raw[:], w1.rearrange("(p j) c -> p j c", j=PACK))
         all_words = keep.tile([P, T], I32, name="all_words", tag="words_then_w2", align_bytes=64)
         nc.sync.dma_start(all_words[:], x_words[0].rearrange("p n t -> p (n t)").bitcast(I32))
-
-        w1_rows = w1.rearrange("(p j) c -> p j c", j=PACK)
-        w1_raw = []
-        for half in range(2):
-            raw = keep.tile([P, PACK, H // 2], F32, name=f"w1_raw{half}")
-            nc.sync.dma_start(raw[:], w1_rows[:, :, half * (H // 2) : (half + 1) * (H // 2)])
-            w1_raw.append(raw)
         w2_raw = keep.tile([P, PACK, N], F32, name="w2_raw")
         nc.sync.dma_start(w2_raw[:], w2.rearrange("(p j) c -> p j c", j=PACK))
 
@@ -67,33 +63,30 @@ def tile_picked_dconv_silu_p_kernel(tc, x_words, x_scales, w1, w2, taps, offs, o
 
         x_scale = keep.tile([P, S], U8, name="x_scale", align_bytes=64)
         nc.vector.tensor_copy(x_scale[:], all_scales[:].indirect(offsets[:]))
-        x_code = []
+        x_code = {}
 
-        def gather_words(half, tag):
-            code = keep.tile([P, S // 2], U32, name=f"x_code{half}", tag=tag, align_bytes=64)
-            entries = offsets[:, half * S // 32 : (half + 1) * S // 32]
+        def gather_words(first, count, tag):
+            code = keep.tile([P, count], U32, name=f"x_code{first}", tag=tag, align_bytes=64)
+            entries = offsets[:, first // 16 : (first + count) // 16]
             nc.vector.tensor_copy(code[:], all_words[:].bitcast(U32).indirect(entries))
-            x_code.append(code)
+            x_code[first] = code
 
-        gather_words(0, "scales_then_codes")
+        def codes(j, width):
+            first = 0 if j < EARLY else EARLY
+            return x_code[first][:, j - first : j - first + width]
+
 
         w1_bf = keep.tile([P, PACK * H], BF16, name="w1_bf", tag="w_bf", align_bytes=64)
         w1_dst = w1_bf[:].rearrange("p (t m j) -> p m j t", t=PACK, j=PACK)
-        w1_src = [raw[:].rearrange("p j (m t) -> p m j t", t=PACK) for raw in w1_raw]
-        nc.scalar.copy(w1_dst[:, 0:64], w1_src[0])
-        nc.scalar.copy(w1_dst[:, 64:80], w1_src[1][:, 0:16])
-        nc.vector.tensor_copy(w1_dst[:, 80:128], w1_src[1][:, 16:64])
+        w1_src = w1_raw[:].rearrange("p j (m t) -> p m j t", t=PACK)
+        nc.scalar.copy(w1_dst[:, 0:48], w1_src[:, 0:48])
+        nc.vector.tensor_copy(w1_dst[:, 48:128], w1_src[:, 48:128])
         w1_code = keep.tile([P, H], U32, name="w1_code", align_bytes=64)
         w1_scale = keep.tile([P, H], U8, name="w1_scale", align_bytes=64)
-        for t in range(PACK):
-            cols = slice(t * P, (t + 1) * P)
-            nc.vector.quantize_mx(
-                out=w1_code[:, cols].bitcast(FP8X4),
-                scales=w1_scale[:, cols],
-                in_=w1_bf[:, t * P * PACK : (t + 1) * P * PACK],
-            )
+        nc.vector.quantize_mx(out=w1_code[:].bitcast(FP8X4), scales=w1_scale[:], in_=w1_bf[:])
 
-        gather_words(1, "w_bf")
+        gather_words(0, EARLY, "early_codes")
+        gather_words(EARLY, S - EARLY, "late_codes")
 
         w2_bf = keep.tile([P, PACK * N], BF16, name="w2_bf", tag="words_then_w2", align_bytes=64)
         w2_code = keep.tile([P, N], U32, name="w2_code", align_bytes=64)
@@ -105,6 +98,8 @@ def tile_picked_dconv_silu_p_kernel(tc, x_words, x_scales, w1, w2, taps, offs, o
                 w2_raw[:].rearrange("p j c -> p c j"),
                 1.0, 0.0, MULT, ADD,
             )
+
+        def quantise_w2():
             nc.vector.quantize_mx(out=w2_code[:].bitcast(FP8X4), scales=w2_scale[:], in_=w2_bf[:])
 
         out_rows = out.rearrange("(h p) s -> p h s", p=P)
@@ -120,7 +115,7 @@ def tile_picked_dconv_silu_p_kernel(tc, x_words, x_scales, w1, w2, taps, offs, o
                         out=h[:, a : a + width],
                         lhsT=w1_code[:, cols].bitcast(FP8X4),
                         lhsT_scale=w1_scale[:, cols],
-                        rhs=x_code[j0 // (S // 2)][:, j0 % (S // 2) + a : j0 % (S // 2) + a + width].bitcast(FP8X4),
+                        rhs=codes(j0 + a, width).bitcast(FP8X4),
                         rhs_scale=x_scale[:, j0 + a : j0 + a + width],
                         start=True,
                         stop=True,
@@ -184,6 +179,8 @@ def tile_picked_dconv_silu_p_kernel(tc, x_words, x_scales, w1, w2, taps, offs, o
             convolve_pair(j0, parts, (0, 1), conv)
             if j0 == 0:
                 prepare_w2()
+            if j0 == sum(CHUNKS[0]):
+                quantise_w2()
             for args in pending[:1]:
                 finish(*args)
             convolve_pair(j0, parts, (2, 3), conv)

@@ -18,10 +18,16 @@ ADD = mybir.AluOpType.add
 
 P = 128
 PACK = 4
+QUADRANT = 32
+LIST_ROWS = 16
+LINE = 4
 HALO = D - 1
-EARLY = 384
-CHUNKS = ((128,), (256, 128), (256, 128), (128,))
-VECTOR_COPIES = (768,)
+
+CHUNKS = ((256,), (256, 128), (128, 128), (128,))
+EARLY = sum(CHUNKS[0])
+W1_ON_SCALAR = 48
+H_BANKS, OUT_BANKS = 6, 2
+RING = 3
 
 
 def spans(widths):
@@ -32,19 +38,22 @@ def tile_picked_dconv_silu_p_kernel(tc, x_words, x_scales, w1, w2, taps, offs, o
     nc = tc.nc
     with ExitStack() as ctx:
         keep = ctx.enter_context(tc.tile_pool(name="keep", bufs=1))
-        ring = ctx.enter_context(tc.tile_pool(name="ring", bufs=3))
-        psum_h = ctx.enter_context(tc.psum_pool(name="psum_h", bufs=6))
-        psum_o = ctx.enter_context(tc.psum_pool(name="psum_o", bufs=2))
+        ring = ctx.enter_context(tc.tile_pool(name="ring", bufs=RING))
+        psum_h = ctx.enter_context(tc.psum_pool(name="psum_h", bufs=H_BANKS))
+        psum_o = ctx.enter_context(tc.psum_pool(name="psum_o", bufs=OUT_BANKS))
 
-        offsets = keep.tile([P, S // 16], U16, name="offsets")
+        offsets = keep.tile([P, S // LIST_ROWS], U16, name="offsets")
         nc.sync.dma_start(offsets[:], offs)
 
         all_scales = keep.tile([P, T], U8, name="all_scales", align_bytes=64)
         nc.gpsimd.memset(all_scales[:].bitcast(I32), 0)
         tap = keep.tile([P, PACK * D], F32, name="tap")
         nc.sync.dma_start(tap[:], taps.rearrange("(p t) d -> p (t d)", t=PACK))
-        for q in range(4):
-            nc.sync.dma_start(all_scales[32 * q : 32 * q + 4, :].bitcast(I32), x_scales[0, 4 * q : 4 * q + 4, :].bitcast(I32))
+        for q in range(P // QUADRANT):
+            nc.sync.dma_start(
+                all_scales[QUADRANT * q : QUADRANT * q + 4, :].bitcast(I32),
+                x_scales[0, 4 * q : 4 * q + 4, :].bitcast(I32),
+            )
 
         w1_raw = keep.tile([P, PACK, H], F32, name="w1_raw")
         nc.sync.dma_start(w1_raw[:], w1.rearrange("(p j) c -> p j c", j=PACK))
@@ -57,82 +66,78 @@ def tile_picked_dconv_silu_p_kernel(tc, x_words, x_scales, w1, w2, taps, offs, o
         nc.vector.memset(zero[:], 0.0)
         acc = []
         for t in range(PACK):
-            a = keep.tile([P, S + HALO], F32, name=f"acc{t}")
-            nc.scalar.activation(a[:, 0:HALO], zero[:], ACT.Silu)
-            acc.append(a)
+            row = keep.tile([P, S + HALO], F32, name=f"acc{t}")
+            nc.scalar.activation(row[:, 0:HALO], zero[:], ACT.Silu)
+            acc.append(row)
 
         x_scale = keep.tile([P, S], U8, name="x_scale", align_bytes=64)
         nc.vector.tensor_copy(x_scale[:], all_scales[:].indirect(offsets[:]))
-        x_code = {}
 
-        def gather_words(first, count, tag):
-            code = keep.tile([P, count], U32, name=f"x_code{first}", tag=tag, align_bytes=64)
-            entries = offsets[:, first // 16 : (first + count) // 16]
-            nc.vector.tensor_copy(code[:], all_words[:].bitcast(U32).indirect(entries))
-            x_code[first] = code
-
-        def codes(j, width):
-            first = 0 if j < EARLY else EARLY
-            return x_code[first][:, j - first : j - first + width]
-
-
-        w1_bf = keep.tile([P, PACK * H], BF16, name="w1_bf", tag="w_bf", align_bytes=64)
+        w1_bf = keep.tile([P, PACK * H], BF16, name="w1_bf", align_bytes=64)
         w1_dst = w1_bf[:].rearrange("p (t m j) -> p m j t", t=PACK, j=PACK)
         w1_src = w1_raw[:].rearrange("p j (m t) -> p m j t", t=PACK)
-        nc.scalar.copy(w1_dst[:, 0:48], w1_src[:, 0:48])
-        nc.vector.tensor_copy(w1_dst[:, 48:128], w1_src[:, 48:128])
+        nc.scalar.copy(w1_dst[:, 0:W1_ON_SCALAR], w1_src[:, 0:W1_ON_SCALAR])
+        nc.vector.tensor_copy(w1_dst[:, W1_ON_SCALAR:P], w1_src[:, W1_ON_SCALAR:P])
         w1_code = keep.tile([P, H], U32, name="w1_code", align_bytes=64)
         w1_scale = keep.tile([P, H], U8, name="w1_scale", align_bytes=64)
         nc.vector.quantize_mx(out=w1_code[:].bitcast(FP8X4), scales=w1_scale[:], in_=w1_bf[:])
 
-        gather_words(0, EARLY, "early_codes")
-        gather_words(EARLY, S - EARLY, "late_codes")
+        x_code = {}
+        for first, count in spans((EARLY, S - EARLY)):
+            picked = keep.tile([P, count], U32, name=f"x_code{first}", align_bytes=64)
+            entries = offsets[:, first // LIST_ROWS : (first + count) // LIST_ROWS]
+            nc.vector.tensor_copy(picked[:], all_words[:].bitcast(U32).indirect(entries))
+            x_code[first] = picked
+
+        def picked_words(j0, width):
+            first = 0 if j0 < EARLY else EARLY
+            return x_code[first][:, j0 - first : j0 - first + width]
 
         w2_bf = keep.tile([P, PACK * N], BF16, name="w2_bf", tag="words_then_w2", align_bytes=64)
         w2_code = keep.tile([P, N], U32, name="w2_code", align_bytes=64)
         w2_scale = keep.tile([P, N], U8, name="w2_scale", align_bytes=64)
 
-        def prepare_w2():
+        def round_w2():
             nc.gpsimd.tensor_scalar(
                 w2_bf[:].rearrange("p (c j) -> p c j", j=PACK),
                 w2_raw[:].rearrange("p j c -> p c j"),
-                1.0, 0.0, MULT, ADD,
+                1.0,
+                0.0,
+                MULT,
+                ADD,
             )
 
-        def quantise_w2():
-            nc.vector.quantize_mx(out=w2_code[:].bitcast(FP8X4), scales=w2_scale[:], in_=w2_bf[:])
+        def tap_column(t, d):
+            return tap[:, D * t + d : D * t + d + 1]
 
-        out_rows = out.rearrange("(h p) s -> p h s", p=P)
-
-        def convolve_pair(j0, parts, pair, conv):
-            n = sum(parts)
-            banks = {}
+        def convolve_pair(j0, widths, pair, u):
+            n = sum(widths)
+            h = {}
             for t in pair:
-                h = psum_h.tile([P, n], F32, name="h", tag="h")
+                h[t] = psum_h.tile([P, n], F32, name="h", tag="h")
                 cols = slice(t * P, (t + 1) * P)
-                for a, width in spans(parts):
+                for a, width in spans(widths):
                     nc.tensor.matmul_mx(
-                        out=h[:, a : a + width],
+                        out=h[t][:, a : a + width],
                         lhsT=w1_code[:, cols].bitcast(FP8X4),
                         lhsT_scale=w1_scale[:, cols],
-                        rhs=codes(j0 + a, width).bitcast(FP8X4),
+                        rhs=picked_words(j0 + a, width).bitcast(FP8X4),
                         rhs_scale=x_scale[:, j0 + a : j0 + a + width],
                         start=True,
                         stop=True,
                     )
-                nc.scalar.activation(acc[t][:, j0 + 2 : j0 + n + 2], h[:], ACT.Copy, scale=tap[:, D * t + 2 : D * t + 3])
-                banks[t] = h
+                nc.scalar.activation(acc[t][:, j0 + 2 : j0 + n + 2], h[t][:], ACT.Copy, scale=tap_column(t, 2))
             for t in pair:
-                part = acc[t][:, j0 + 1 : j0 + n + 1]
-                nc.vector.scalar_tensor_tensor(part, banks[t][:], tap[:, D * t + 1 : D * t + 2], part, MULT, ADD)
+                shifted = acc[t][:, j0 + 1 : j0 + n + 1]
+                nc.vector.scalar_tensor_tensor(shifted, h[t][:], tap_column(t, 1), shifted, MULT, ADD)
             for t in pair:
-                nc.vector.scalar_tensor_tensor(conv[:, t, :], banks[t][:], tap[:, D * t : D * t + 1], acc[t][:, j0 : j0 + n], MULT, ADD)
+                nc.vector.scalar_tensor_tensor(u[:, t, :], h[t][:], tap_column(t, 0), acc[t][:, j0 : j0 + n], MULT, ADD)
 
-        def activate_and_quantise(n, conv):
+        def activate_and_quantise(n, u):
             z = ring.tile([P, n * PACK], BF16, name="z", tag="z", align_bytes=64)
             nc.scalar.activation(
-                z[:].rearrange("p (c i t) -> p c t i", i=4, t=PACK),
-                conv.rearrange("p t (c i) -> p c t i", i=4),
+                z[:].rearrange("p (c i t) -> p c t i", i=LINE, t=PACK),
+                u.rearrange("p t (c i) -> p c t i", i=LINE),
                 ACT.Silu,
             )
             z_code = ring.tile([P, n], U32, name="z_code", tag="z_code", align_bytes=64)
@@ -152,40 +157,40 @@ def tile_picked_dconv_silu_p_kernel(tc, x_words, x_scales, w1, w2, taps, offs, o
                 stop=True,
             )
 
-        def project_and_store(j0, n, z_code, z_scale, copy):
-            o = psum_o.tile([P, 2, n], F32, name="o", tag="o")
-            for half in range(2):
-                second_product(o[:, half, :], half, z_code, z_scale)
-            res = keep.tile([P, 2, n], F32, name=f"res{j0}")
-            copy(res[:], o[:])
-            nc.sync.dma_start(out_rows[:, :, j0 : j0 + n], res[:])
+        out_rows = out.rearrange("(half p) s -> p half s", p=P)
+        last_width = CHUNKS[-1][-1]
 
-        def finish(j0, n, conv):
-            z_code, z_scale = activate_and_quantise(n, conv)
-            if j0 + n < S:
-                copy = nc.vector.tensor_copy if j0 in VECTOR_COPIES else nc.scalar.copy
-                project_and_store(j0, n, z_code, z_scale, copy)
-            else:
-                for half, copy, queue in ((0, nc.scalar.copy, nc.scalar), (1, nc.vector.tensor_copy, nc.sync)):
-                    o = psum_o.tile([P, n], F32, name="o_last", tag="o")
-                    second_product(o[:], half, z_code, z_scale)
-                    res = keep.tile([P, n], F32, name=f"res_last{half}")
-                    copy(res[:], o[:])
-                    queue.dma_start(out_rows[:, half, j0 : j0 + n], res[:])
+        def finish(j0, n, u):
+            z_code, z_scale = activate_and_quantise(n, u)
+            product = psum_o.tile([P, 2, n], F32, name="product", tag="product")
+            for half in range(2):
+                second_product(product[:, half, :], half, z_code, z_scale)
+            result = keep.tile([P, 2, n], F32, name=f"result{j0}")
+            copy = nc.vector.tensor_copy if j0 + n == S - last_width else nc.scalar.copy
+            copy(result[:], product[:])
+            nc.sync.dma_start(out_rows[:, :, j0 : j0 + n], result[:])
+
+        def finish_last(j0, n, u):
+            z_code, z_scale = activate_and_quantise(n, u)
+            for half, copy, queue in ((0, nc.scalar.copy, nc.scalar), (1, nc.vector.tensor_copy, nc.sync)):
+                product = psum_h.tile([P, n], F32, name="last_product", tag="h")
+                second_product(product[:], half, z_code, z_scale)
+                result = keep.tile([P, n], F32, name=f"last_result{half}")
+                copy(result[:], product[:])
+                queue.dma_start(out_rows[:, half, j0 : j0 + n], result[:])
 
         pending = []
-        for parts, (j0, n) in zip(CHUNKS, spans([sum(parts) for parts in CHUNKS])):
-            conv = ring.tile([P, PACK, n], F32, name="conv", tag="conv")
-            convolve_pair(j0, parts, (0, 1), conv)
-            if j0 == 0:
-                prepare_w2()
-            if j0 == sum(CHUNKS[0]):
-                quantise_w2()
-            for args in pending[:1]:
-                finish(*args)
-            convolve_pair(j0, parts, (2, 3), conv)
-            for args in pending[1:]:
-                finish(*args)
-            pending = [(j0 + a, width, conv[:, :, a : a + width]) for a, width in spans(parts)]
-        for args in pending:
-            finish(*args)
+        for c, (j0, n) in enumerate(spans([sum(widths) for widths in CHUNKS])):
+            u = ring.tile([P, PACK, n], F32, name="u", tag="u")
+            convolve_pair(j0, CHUNKS[c], (0, 1), u)
+            if c == 0:
+                round_w2()
+            if c == 1:
+                nc.vector.quantize_mx(out=w2_code[:].bitcast(FP8X4), scales=w2_scale[:], in_=w2_bf[:])
+            for piece in pending[:1]:
+                finish(*piece)
+            convolve_pair(j0, CHUNKS[c], (2, 3), u)
+            for piece in pending[1:]:
+                finish(*piece)
+            pending = [(j0 + a, width, u[:, :, a : a + width]) for a, width in spans(CHUNKS[c])]
+        finish_last(*pending[0])

@@ -25,7 +25,7 @@ HALO = D - 1
 
 CHUNKS = ((256,), (256, 128), (128, 128), (128,))
 EARLY = sum(CHUNKS[0])
-W1_ON_SCALAR = 48
+W1_ON_SCALAR = 64
 H_BANKS, OUT_BANKS = 6, 2
 RING = 3
 
@@ -166,7 +166,7 @@ def tile_picked_dconv_silu_p_kernel(tc, x_words, x_scales, w1, w2, taps, offs, o
             for half in range(2):
                 second_product(product[:, half, :], half, z_code, z_scale)
             result = keep.tile([P, 2, n], F32, name=f"result{j0}")
-            copy = nc.vector.tensor_copy if j0 + n == S - last_width else nc.scalar.copy
+            copy = nc.vector.tensor_copy if n == last_width else nc.scalar.copy
             copy(result[:], product[:])
             nc.sync.dma_start(out_rows[:, :, j0 : j0 + n], result[:])
 

@@ -23,11 +23,15 @@ LIST_ROWS = 16
 LINE = 4
 HALO = D - 1
 
-CHUNKS = ((256,), (256, 128), (128, 128), (128,))
-EARLY = sum(CHUNKS[0])
-W1_ON_SCALAR = 64
-H_BANKS, OUT_BANKS = 6, 2
+CHUNKS = (((256,),), ((256,), (128, 128)), ((128,), (64, 64)))
+VECTOR_COPIES = 1
+GPSIMD_TILES = ()
+W1_ON_SCALAR = 80
 RING = 3
+
+
+PIECES = [width for chunk in CHUNKS for step in chunk for width in step]
+CHUNK_WIDTHS = [sum(sum(step) for step in chunk) for chunk in CHUNKS]
 
 
 def spans(widths):
@@ -39,26 +43,25 @@ def tile_picked_dconv_silu_p_kernel(tc, x_words, x_scales, w1, w2, taps, offs, o
     with ExitStack() as ctx:
         keep = ctx.enter_context(tc.tile_pool(name="keep", bufs=1))
         ring = ctx.enter_context(tc.tile_pool(name="ring", bufs=RING))
-        psum_h = ctx.enter_context(tc.psum_pool(name="psum_h", bufs=H_BANKS))
-        psum_o = ctx.enter_context(tc.psum_pool(name="psum_o", bufs=OUT_BANKS))
+        codes = ctx.enter_context(tc.tile_pool(name="codes", bufs=len(PIECES)))
+        psum = ctx.enter_context(tc.psum_pool(name="psum", bufs=1))
 
+        w1_raw = keep.tile([P, PACK, H], F32, name="w1_raw")
+        w1_rows = w1.rearrange("(p j) c -> p j c", j=PACK)
+        nc.sync.dma_start(w1_raw[:, 0:2, :], w1_rows[:, 0:2, :])
         offsets = keep.tile([P, S // LIST_ROWS], U16, name="offsets")
         nc.sync.dma_start(offsets[:], offs)
 
         all_scales = keep.tile([P, T], U8, name="all_scales", align_bytes=64)
         nc.gpsimd.memset(all_scales[:].bitcast(I32), 0)
-        tap = keep.tile([P, PACK * D], F32, name="tap")
-        nc.sync.dma_start(tap[:], taps.rearrange("(p t) d -> p (t d)", t=PACK))
-        for q in range(P // QUADRANT):
-            nc.sync.dma_start(
-                all_scales[QUADRANT * q : QUADRANT * q + 4, :].bitcast(I32),
-                x_scales[0, 4 * q : 4 * q + 4, :].bitcast(I32),
-            )
+        for r in range(4):
+            nc.sync.dma_start(all_scales[r:P:QUADRANT, :].bitcast(I32), x_scales[0, r:16:4, :].bitcast(I32))
 
-        w1_raw = keep.tile([P, PACK, H], F32, name="w1_raw")
-        nc.sync.dma_start(w1_raw[:], w1.rearrange("(p j) c -> p j c", j=PACK))
+        nc.sync.dma_start(w1_raw[:, 2:4, :], w1_rows[:, 2:4, :])
         all_words = keep.tile([P, T], I32, name="all_words", tag="words_then_w2", align_bytes=64)
         nc.sync.dma_start(all_words[:], x_words[0].rearrange("p n t -> p (n t)").bitcast(I32))
+        tap = keep.tile([P, PACK * D], F32, name="tap")
+        nc.sync.dma_start(tap[:], taps.rearrange("(p t) d -> p (t d)", t=PACK))
         w2_raw = keep.tile([P, PACK, N], F32, name="w2_raw")
         nc.sync.dma_start(w2_raw[:], w2.rearrange("(p j) c -> p j c", j=PACK))
 
@@ -82,16 +85,16 @@ def tile_picked_dconv_silu_p_kernel(tc, x_words, x_scales, w1, w2, taps, offs, o
         w1_scale = keep.tile([P, H], U8, name="w1_scale", align_bytes=64)
         nc.vector.quantize_mx(out=w1_code[:].bitcast(FP8X4), scales=w1_scale[:], in_=w1_bf[:])
 
-        x_code = {}
-        for first, count in spans((EARLY, S - EARLY)):
+        x_code = []
+        for first, count in spans(CHUNK_WIDTHS):
             picked = keep.tile([P, count], U32, name=f"x_code{first}", align_bytes=64)
             entries = offsets[:, first // LIST_ROWS : (first + count) // LIST_ROWS]
             nc.vector.tensor_copy(picked[:], all_words[:].bitcast(U32).indirect(entries))
-            x_code[first] = picked
+            x_code.append((first, count, picked))
 
         def picked_words(j0, width):
-            first = 0 if j0 < EARLY else EARLY
-            return x_code[first][:, j0 - first : j0 - first + width]
+            first, picked = [(f, tile) for f, count, tile in x_code if f <= j0 < f + count][0]
+            return picked[:, j0 - first : j0 - first + width]
 
         w2_bf = keep.tile([P, PACK * N], BF16, name="w2_bf", tag="words_then_w2", align_bytes=64)
         w2_code = keep.tile([P, N], U32, name="w2_code", align_bytes=64)
@@ -110,28 +113,36 @@ def tile_picked_dconv_silu_p_kernel(tc, x_words, x_scales, w1, w2, taps, offs, o
         def tap_column(t, d):
             return tap[:, D * t + d : D * t + d + 1]
 
-        def convolve_pair(j0, widths, pair, u):
-            n = sum(widths)
-            h = {}
-            for t in pair:
-                h[t] = psum_h.tile([P, n], F32, name="h", tag="h")
-                cols = slice(t * P, (t + 1) * P)
-                for a, width in spans(widths):
-                    nc.tensor.matmul_mx(
-                        out=h[t][:, a : a + width],
-                        lhsT=w1_code[:, cols].bitcast(FP8X4),
-                        lhsT_scale=w1_scale[:, cols],
-                        rhs=picked_words(j0 + a, width).bitcast(FP8X4),
-                        rhs_scale=x_scale[:, j0 + a : j0 + a + width],
-                        start=True,
-                        stop=True,
-                    )
-                nc.scalar.activation(acc[t][:, j0 + 2 : j0 + n + 2], h[t][:], ACT.Copy, scale=tap_column(t, 2))
-            for t in pair:
+        def on_gpsimd(c, t):
+            return c == len(CHUNKS) - 1 and t in GPSIMD_TILES
+
+        def first_product(c, t):
+            j0, n = chunks[c]
+            h = psum.tile([P, n], F32, name="h", tag=f"bank{PACK * (c % 2) + t}")
+            cols = slice(t * P, (t + 1) * P)
+            nc.tensor.matmul_mx(
+                out=h[:],
+                lhsT=w1_code[:, cols].bitcast(FP8X4),
+                lhsT_scale=w1_scale[:, cols],
+                rhs=picked_words(j0, n).bitcast(FP8X4),
+                rhs_scale=x_scale[:, j0 : j0 + n],
+                start=True,
+                stop=True,
+            )
+            nc.scalar.activation(acc[t][:, j0 + 2 : j0 + n + 2], h[:], ACT.Copy, scale=tap_column(t, 2))
+            if on_gpsimd(c, t):
+                term = keep.tile([P, n], F32, name=f"term{t}")
+                nc.scalar.activation(term[:], h[:], ACT.Copy, scale=tap_column(t, 1))
                 shifted = acc[t][:, j0 + 1 : j0 + n + 1]
-                nc.vector.scalar_tensor_tensor(shifted, h[t][:], tap_column(t, 1), shifted, MULT, ADD)
-            for t in pair:
-                nc.vector.scalar_tensor_tensor(u[:, t, :], h[t][:], tap_column(t, 0), acc[t][:, j0 : j0 + n], MULT, ADD)
+                nc.gpsimd.tensor_tensor(shifted, shifted, term[:], ADD)
+            return h
+
+        def add_tap1(j0, n, t, h):
+            shifted = acc[t][:, j0 + 1 : j0 + n + 1]
+            nc.vector.scalar_tensor_tensor(shifted, h, tap_column(t, 1), shifted, MULT, ADD)
+
+        def add_tap0(j0, n, t, h, u):
+            nc.vector.scalar_tensor_tensor(u, h, tap_column(t, 0), acc[t][:, j0 : j0 + n], MULT, ADD)
 
         def activate_and_quantise(n, u):
             z = ring.tile([P, n * PACK], BF16, name="z", tag="z", align_bytes=64)
@@ -140,10 +151,10 @@ def tile_picked_dconv_silu_p_kernel(tc, x_words, x_scales, w1, w2, taps, offs, o
                 u.rearrange("p t (c i) -> p c t i", i=LINE),
                 ACT.Silu,
             )
-            z_code = ring.tile([P, n], U32, name="z_code", tag="z_code", align_bytes=64)
-            z_scale = ring.tile([P, n], U8, name="z_scale", tag="z_scale", align_bytes=64)
+            z_code = codes.tile([P, n], U32, name="z_code", tag="z_code", align_bytes=64)
+            z_scale = codes.tile([P, n], U8, name="z_scale", tag="z_scale", align_bytes=64)
             nc.vector.quantize_mx(out=z_code[:].bitcast(FP8X4), scales=z_scale[:], in_=z[:])
-            return z_code, z_scale
+            return n, z_code, z_scale
 
         def second_product(dst, half, z_code, z_scale):
             cols = slice(half * P, (half + 1) * P)
@@ -158,39 +169,54 @@ def tile_picked_dconv_silu_p_kernel(tc, x_words, x_scales, w1, w2, taps, offs, o
             )
 
         out_rows = out.rearrange("(half p) s -> p half s", p=P)
-        last_width = CHUNKS[-1][-1]
 
-        def finish(j0, n, u):
-            z_code, z_scale = activate_and_quantise(n, u)
-            product = psum_o.tile([P, 2, n], F32, name="product", tag="product")
+        starts = [j0 for j0, n in spans(PIECES)]
+
+        def finish(j0, n, z_code, z_scale):
+            product = psum.tile([P, 2, n], F32, name="product", tag=f"bank{PACK + starts.index(j0) % PACK}")
             for half in range(2):
                 second_product(product[:, half, :], half, z_code, z_scale)
             result = keep.tile([P, 2, n], F32, name=f"result{j0}")
-            copy = nc.vector.tensor_copy if n == last_width else nc.scalar.copy
+            copy = nc.vector.tensor_copy if j0 in starts[-1 - VECTOR_COPIES :] else nc.scalar.copy
             copy(result[:], product[:])
             nc.sync.dma_start(out_rows[:, :, j0 : j0 + n], result[:])
 
-        def finish_last(j0, n, u):
-            z_code, z_scale = activate_and_quantise(n, u)
+        def finish_last(j0, n, z_code, z_scale):
             for half, copy, queue in ((0, nc.scalar.copy, nc.scalar), (1, nc.vector.tensor_copy, nc.sync)):
-                product = psum_h.tile([P, n], F32, name="last_product", tag="h")
+                product = psum.tile([P, n], F32, name="last_product", tag=f"bank{half}")
                 second_product(product[:], half, z_code, z_scale)
                 result = keep.tile([P, n], F32, name=f"last_result{half}")
                 copy(result[:], product[:])
                 queue.dma_start(out_rows[:, half, j0 : j0 + n], result[:])
 
-        pending = []
-        for c, (j0, n) in enumerate(spans([sum(widths) for widths in CHUNKS])):
+        def convolve(c, a, widths):
+            j0, n = chunks[c][0] + a, sum(widths)
             u = ring.tile([P, PACK, n], F32, name="u", tag="u")
-            convolve_pair(j0, CHUNKS[c], (0, 1), u)
-            if c == 0:
-                round_w2()
-            if c == 1:
-                nc.vector.quantize_mx(out=w2_code[:].bitcast(FP8X4), scales=w2_scale[:], in_=w2_bf[:])
-            for piece in pending[:1]:
+            for group in ((0, 1), (2, 3)) if n > P else ((0, 1, 2, 3),):
+                for t in group:
+                    if not on_gpsimd(c, t):
+                        add_tap1(j0, n, t, h[c, t][:, a : a + n])
+                for t in group:
+                    add_tap0(j0, n, t, h[c, t][:, a : a + n], u[:, t, :])
+            return [(j0 + b, *activate_and_quantise(width, u[:, :, b : b + width])) for b, width in spans(widths)]
+
+        def steps(c):
+            return zip([a for a, n in spans([sum(step) for step in CHUNKS[c]])], CHUNKS[c])
+
+        chunks = spans(CHUNK_WIDTHS)
+        h = {(c, t): first_product(c, t) for c in range(2) for t in range(PACK)}
+        round_w2()
+        pending = convolve(0, 0, CHUNKS[0][0])
+        for t in range(PACK):
+            h[2, t] = first_product(2, t)
+        nc.vector.quantize_mx(out=w2_code[:].bitcast(FP8X4), scales=w2_scale[:], in_=w2_bf[:])
+        for a, widths in steps(1):
+            pending = pending + convolve(1, a, widths)
+        for a, widths in steps(2):
+            quantised = convolve(2, a, widths)
+            for piece in pending:
                 finish(*piece)
-            convolve_pair(j0, CHUNKS[c], (2, 3), u)
-            for piece in pending[1:]:
-                finish(*piece)
-            pending = [(j0 + a, width, u[:, :, a : a + width]) for a, width in spans(CHUNKS[c])]
-        finish_last(*pending[0])
+            pending = quantised
+        for piece in pending[:-1]:
+            finish(*piece)
+        finish_last(*pending[-1])

@@ -23,15 +23,14 @@ LIST_ROWS = 16
 LINE = 4
 HALO = D - 1
 
-CHUNKS = (((256,),), ((256,), (128, 128)), ((128,), (64, 64)))
-VECTOR_COPIES = 1
-GPSIMD_TILES = ()
+CHUNKS = ((256,), (256, 256), (128, 128))
+GPSIMD_TILES = (0, 1, 2)
 W1_ON_SCALAR = 80
-RING = 3
+RING = 5
 
 
-PIECES = [width for chunk in CHUNKS for step in chunk for width in step]
-CHUNK_WIDTHS = [sum(sum(step) for step in chunk) for chunk in CHUNKS]
+PIECES = [width for chunk in CHUNKS for width in chunk]
+CHUNK_WIDTHS = [sum(chunk) for chunk in CHUNKS]
 
 
 def spans(widths):
@@ -43,12 +42,11 @@ def tile_picked_dconv_silu_p_kernel(tc, x_words, x_scales, w1, w2, taps, offs, o
     with ExitStack() as ctx:
         keep = ctx.enter_context(tc.tile_pool(name="keep", bufs=1))
         ring = ctx.enter_context(tc.tile_pool(name="ring", bufs=RING))
-        codes = ctx.enter_context(tc.tile_pool(name="codes", bufs=len(PIECES)))
         psum = ctx.enter_context(tc.psum_pool(name="psum", bufs=1))
 
         w1_raw = keep.tile([P, PACK, H], F32, name="w1_raw")
         w1_rows = w1.rearrange("(p j) c -> p j c", j=PACK)
-        nc.sync.dma_start(w1_raw[:, 0:2, :], w1_rows[:, 0:2, :])
+        nc.sync.dma_start(w1_raw[:, 0:1, :], w1_rows[:, 0:1, :])
         offsets = keep.tile([P, S // LIST_ROWS], U16, name="offsets")
         nc.sync.dma_start(offsets[:], offs)
 
@@ -57,7 +55,7 @@ def tile_picked_dconv_silu_p_kernel(tc, x_words, x_scales, w1, w2, taps, offs, o
         for r in range(4):
             nc.sync.dma_start(all_scales[r:P:QUADRANT, :].bitcast(I32), x_scales[0, r:16:4, :].bitcast(I32))
 
-        nc.sync.dma_start(w1_raw[:, 2:4, :], w1_rows[:, 2:4, :])
+        nc.sync.dma_start(w1_raw[:, 1:4, :], w1_rows[:, 1:4, :])
         all_words = keep.tile([P, T], I32, name="all_words", tag="words_then_w2", align_bytes=64)
         nc.sync.dma_start(all_words[:], x_words[0].rearrange("p n t -> p (n t)").bitcast(I32))
         tap = keep.tile([P, PACK * D], F32, name="tap")
@@ -113,15 +111,19 @@ def tile_picked_dconv_silu_p_kernel(tc, x_words, x_scales, w1, w2, taps, offs, o
         def tap_column(t, d):
             return tap[:, D * t + d : D * t + d + 1]
 
+        term = {}
+        for t in GPSIMD_TILES:
+            term[t] = keep.tile([P, CHUNK_WIDTHS[-1]], F32, name=f"term{t}")
+            nc.gpsimd.memset(term[t][:, 0:1], 0.0)
+
         def on_gpsimd(c, t):
             return c == len(CHUNKS) - 1 and t in GPSIMD_TILES
 
-        def first_product(c, t):
+        def first_product(c, t, h):
             j0, n = chunks[c]
-            h = psum.tile([P, n], F32, name="h", tag=f"bank{PACK * (c % 2) + t}")
             cols = slice(t * P, (t + 1) * P)
             nc.tensor.matmul_mx(
-                out=h[:],
+                out=h,
                 lhsT=w1_code[:, cols].bitcast(FP8X4),
                 lhsT_scale=w1_scale[:, cols],
                 rhs=picked_words(j0, n).bitcast(FP8X4),
@@ -129,13 +131,12 @@ def tile_picked_dconv_silu_p_kernel(tc, x_words, x_scales, w1, w2, taps, offs, o
                 start=True,
                 stop=True,
             )
-            nc.scalar.activation(acc[t][:, j0 + 2 : j0 + n + 2], h[:], ACT.Copy, scale=tap_column(t, 2))
+
+        def scalar_taps(c, t, h):
+            j0, n = chunks[c]
+            nc.scalar.activation(acc[t][:, j0 + 2 : j0 + n + 2], h, ACT.Copy, scale=tap_column(t, 2))
             if on_gpsimd(c, t):
-                term = keep.tile([P, n], F32, name=f"term{t}")
-                nc.scalar.activation(term[:], h[:], ACT.Copy, scale=tap_column(t, 1))
-                shifted = acc[t][:, j0 + 1 : j0 + n + 1]
-                nc.gpsimd.tensor_tensor(shifted, shifted, term[:], ADD)
-            return h
+                nc.scalar.activation(term[t][:, 1:n], h[:, 0 : n - 1], ACT.Copy, scale=tap_column(t, 1))
 
         def add_tap1(j0, n, t, h):
             shifted = acc[t][:, j0 + 1 : j0 + n + 1]
@@ -144,17 +145,20 @@ def tile_picked_dconv_silu_p_kernel(tc, x_words, x_scales, w1, w2, taps, offs, o
         def add_tap0(j0, n, t, h, u):
             nc.vector.scalar_tensor_tensor(u, h, tap_column(t, 0), acc[t][:, j0 : j0 + n], MULT, ADD)
 
-        def activate_and_quantise(n, u):
+        def activate(n, u):
             z = ring.tile([P, n * PACK], BF16, name="z", tag="z", align_bytes=64)
             nc.scalar.activation(
                 z[:].rearrange("p (c i t) -> p c t i", i=LINE, t=PACK),
-                u.rearrange("p t (c i) -> p c t i", i=LINE),
+                u[:].rearrange("p t (c i) -> p c t i", i=LINE),
                 ACT.Silu,
             )
-            z_code = codes.tile([P, n], U32, name="z_code", tag="z_code", align_bytes=64)
-            z_scale = codes.tile([P, n], U8, name="z_scale", tag="z_scale", align_bytes=64)
+            return z
+
+        def quantise(n, z):
+            z_code = ring.tile([P, n], U32, name="z_code", tag="z_code", align_bytes=64)
+            z_scale = ring.tile([P, n], U8, name="z_scale", tag="z_scale", align_bytes=64)
             nc.vector.quantize_mx(out=z_code[:].bitcast(FP8X4), scales=z_scale[:], in_=z[:])
-            return n, z_code, z_scale
+            return z_code, z_scale
 
         def second_product(dst, half, z_code, z_scale):
             cols = slice(half * P, (half + 1) * P)
@@ -170,53 +174,83 @@ def tile_picked_dconv_silu_p_kernel(tc, x_words, x_scales, w1, w2, taps, offs, o
 
         out_rows = out.rearrange("(half p) s -> p half s", p=P)
 
-        starts = [j0 for j0, n in spans(PIECES)]
+        def finish(k, z, copy):
+            store(k, quantise(PIECES[k], z), copy)
 
-        def finish(j0, n, z_code, z_scale):
-            product = psum.tile([P, 2, n], F32, name="product", tag=f"bank{PACK + starts.index(j0) % PACK}")
+        def store(k, codes, copy):
+            j0, n = pieces[k]
+            z_code, z_scale = codes
+            product = psum.tile([P, 2, n], F32, name="product", tag=f"bank{k % 2}")
             for half in range(2):
                 second_product(product[:, half, :], half, z_code, z_scale)
             result = keep.tile([P, 2, n], F32, name=f"result{j0}")
-            copy = nc.vector.tensor_copy if j0 in starts[-1 - VECTOR_COPIES :] else nc.scalar.copy
             copy(result[:], product[:])
             nc.sync.dma_start(out_rows[:, :, j0 : j0 + n], result[:])
 
-        def finish_last(j0, n, z_code, z_scale):
+        def store_halves(k, codes, first_bank):
+            j0, n = pieces[k]
             for half, copy, queue in ((0, nc.scalar.copy, nc.scalar), (1, nc.vector.tensor_copy, nc.sync)):
-                product = psum.tile([P, n], F32, name="last_product", tag=f"bank{half}")
-                second_product(product[:], half, z_code, z_scale)
-                result = keep.tile([P, n], F32, name=f"last_result{half}")
+                product = psum.tile([P, n], F32, name="half_product", tag=f"bank{first_bank + half}")
+                second_product(product[:], half, *codes)
+                result = keep.tile([P, n], F32, name=f"half_result{k}{half}")
                 copy(result[:], product[:])
                 queue.dma_start(out_rows[:, half, j0 : j0 + n], result[:])
 
-        def convolve(c, a, widths):
-            j0, n = chunks[c][0] + a, sum(widths)
+        def tap1_of_chunk(c):
+            j0, n = chunks[c]
+            for t in range(PACK):
+                if on_gpsimd(c, t):
+                    own = acc[t][:, j0 : j0 + n]
+                    nc.gpsimd.tensor_tensor(own, own, term[t][:], ADD)
+                else:
+                    add_tap1(j0, n, t, h[c, t])
+
+        def tap1_of_piece(c, k):
+            j0, n = pieces[k]
+            a = j0 - chunks[c][0]
+            for t in range(PACK):
+                add_tap1(j0, n, t, h[c, t][:, a : a + n])
+
+        def tap0_of_piece(c, k):
+            j0, n = pieces[k]
+            a = j0 - chunks[c][0]
             u = ring.tile([P, PACK, n], F32, name="u", tag="u")
-            for group in ((0, 1), (2, 3)) if n > P else ((0, 1, 2, 3),):
-                for t in group:
-                    if not on_gpsimd(c, t):
-                        add_tap1(j0, n, t, h[c, t][:, a : a + n])
-                for t in group:
-                    add_tap0(j0, n, t, h[c, t][:, a : a + n], u[:, t, :])
-            return [(j0 + b, *activate_and_quantise(width, u[:, :, b : b + width])) for b, width in spans(widths)]
+            for t in range(PACK):
+                add_tap0(j0, n, t, h[c, t][:, a : a + n], u[:, t, :])
+            return u
 
-        def steps(c):
-            return zip([a for a, n in spans([sum(step) for step in CHUNKS[c]])], CHUNKS[c])
-
-        chunks = spans(CHUNK_WIDTHS)
-        h = {(c, t): first_product(c, t) for c in range(2) for t in range(PACK)}
+        chunks, pieces = spans(CHUNK_WIDTHS), spans(PIECES)
+        h = {}
+        for c in range(2):
+            for t in range(PACK):
+                bank = psum.tile([P, CHUNK_WIDTHS[c]], F32, name="h", tag=f"bank{PACK * c + t}")
+                h[c, t] = bank[:]
+                first_product(c, t, h[c, t])
+                scalar_taps(c, t, h[c, t])
         round_w2()
-        pending = convolve(0, 0, CHUNKS[0][0])
-        for t in range(PACK):
-            h[2, t] = first_product(2, t)
+        tap1_of_chunk(0)
+        z0 = activate(PIECES[0], tap0_of_piece(0, 0))
+        for pair in ((0, 1), (2, 3)):
+            bank = psum.tile([P, 2, CHUNK_WIDTHS[2]], F32, name="h_pair", tag=f"bank{2 + pair[0] // 2}")
+            for t in pair:
+                h[2, t] = bank[:, t % 2, :]
+                first_product(2, t, h[2, t])
+            for t in pair:
+                scalar_taps(2, t, h[2, t])
         nc.vector.quantize_mx(out=w2_code[:].bitcast(FP8X4), scales=w2_scale[:], in_=w2_bf[:])
-        for a, widths in steps(1):
-            pending = pending + convolve(1, a, widths)
-        for a, widths in steps(2):
-            quantised = convolve(2, a, widths)
-            for piece in pending:
-                finish(*piece)
-            pending = quantised
-        for piece in pending[:-1]:
-            finish(*piece)
-        finish_last(*pending[-1])
+        finish(0, z0, nc.scalar.copy)
+        tap1_of_piece(1, 1)
+        z1 = activate(PIECES[1], tap0_of_piece(1, 1))
+        tap1_of_piece(1, 2)
+        z2 = activate(PIECES[2], tap0_of_piece(1, 2))
+        codes1 = quantise(PIECES[1], z1)
+        tap1_of_chunk(2)
+        z3 = activate(PIECES[3], tap0_of_piece(2, 3))
+        z4 = activate(PIECES[4], tap0_of_piece(2, 4))
+        codes2 = quantise(PIECES[2], z2)
+        codes3 = quantise(PIECES[3], z3)
+        codes4 = quantise(PIECES[4], z4)
+        store(1, codes1, nc.vector.tensor_copy)
+        store_halves(2, codes2, 4)
+        store(3, codes3, nc.scalar.copy)
+        store_halves(4, codes4, 6)

@@ -51,7 +51,7 @@ def tile_picked_dconv_silu_p_kernel(tc, x_words, x_scales, w1, w2, taps, offs, o
         nc.sync.dma_start(offsets[:], offs)
 
         all_scales = keep.tile([P, T], U8, name="all_scales", align_bytes=64)
-        nc.gpsimd.memset(all_scales[:].bitcast(I32), 0)
+        nc.vector.memset(all_scales[:].bitcast(I32), 0)
         for r in range(4):
             nc.sync.dma_start(all_scales[r:P:QUADRANT, :].bitcast(I32), x_scales[0, r:16:4, :].bitcast(I32))
 

@@ -25,7 +25,7 @@ HALO = D - 1
 
 CHUNKS = ((256,), (256, 256), (128, 128))
 GPSIMD_TILES = (0, 1, 2)
-W1_ON_SCALAR = 80
+W1_ON_SCALAR = 64
 RING = 5
 
 
@@ -215,7 +215,7 @@ def tile_picked_dconv_silu_p_kernel(tc, x_words, x_scales, w1, w2, taps, offs, o
             j0, n = pieces[k]
             a = j0 - chunks[c][0]
             u = ring.tile([P, PACK, n], F32, name="u", tag="u")
-            for t in range(PACK):
+            for t in sorted(range(PACK), key=lambda t: on_gpsimd(c, t)):
                 add_tap0(j0, n, t, h[c, t][:, a : a + n], u[:, t, :])
             return u
 
@@ -237,9 +237,9 @@ def tile_picked_dconv_silu_p_kernel(tc, x_words, x_scales, w1, w2, taps, offs, o
                 first_product(2, t, h[2, t])
             for t in pair:
                 scalar_taps(2, t, h[2, t])
+        tap1_of_piece(1, 1)
         nc.vector.quantize_mx(out=w2_code[:].bitcast(FP8X4), scales=w2_scale[:], in_=w2_bf[:])
         finish(0, z0, nc.scalar.copy)
-        tap1_of_piece(1, 1)
         z1 = activate(PIECES[1], tap0_of_piece(1, 1))
         tap1_of_piece(1, 2)
         z2 = activate(PIECES[2], tap0_of_piece(1, 2))

@@ -19,18 +19,19 @@ ADD = mybir.AluOpType.add
 P = 128
 PACK = 4
 QUADRANT = 32
+SCALE_ROWS = 4
 LIST_ROWS = 16
 LINE = 4
 HALO = D - 1
+ROW = S + 8
 
 CHUNKS = ((256,), (256, 256), (128, 128))
-GPSIMD_TILES = (0, 1, 2)
-W1_ON_SCALAR = 64
-RING = 5
-
-
 PIECES = [width for chunk in CHUNKS for width in chunk]
 CHUNK_WIDTHS = [sum(chunk) for chunk in CHUNKS]
+LAST = len(CHUNKS) - 1
+GPSIMD_TILES = 3
+W1_ON_SCALAR = 64
+RING = len(PIECES)
 
 
 def spans(widths):
@@ -52,10 +53,11 @@ def tile_picked_dconv_silu_p_kernel(tc, x_words, x_scales, w1, w2, taps, offs, o
 
         all_scales = keep.tile([P, T], U8, name="all_scales", align_bytes=64)
         nc.vector.memset(all_scales[:].bitcast(I32), 0)
-        for r in range(4):
-            nc.sync.dma_start(all_scales[r:P:QUADRANT, :].bitcast(I32), x_scales[0, r:16:4, :].bitcast(I32))
+        for r in range(SCALE_ROWS):
+            rows = x_scales[0, r : K // QUADRANT : SCALE_ROWS, :]
+            nc.sync.dma_start(all_scales[r:P:QUADRANT, :].bitcast(I32), rows.bitcast(I32))
 
-        nc.sync.dma_start(w1_raw[:, 1:4, :], w1_rows[:, 1:4, :])
+        nc.sync.dma_start(w1_raw[:, 1:PACK, :], w1_rows[:, 1:PACK, :])
         all_words = keep.tile([P, T], I32, name="all_words", tag="words_then_w2", align_bytes=64)
         nc.sync.dma_start(all_words[:], x_words[0].rearrange("p n t -> p (n t)").bitcast(I32))
         tap = keep.tile([P, PACK * D], F32, name="tap")
@@ -63,13 +65,10 @@ def tile_picked_dconv_silu_p_kernel(tc, x_words, x_scales, w1, w2, taps, offs, o
         w2_raw = keep.tile([P, PACK, N], F32, name="w2_raw")
         nc.sync.dma_start(w2_raw[:], w2.rearrange("(p j) c -> p j c", j=PACK))
 
-        zero = keep.tile([P, HALO], F32, name="zero")
+        zero = keep.tile([P, PACK, HALO], F32, name="zero")
         nc.vector.memset(zero[:], 0.0)
-        acc = []
-        for t in range(PACK):
-            row = keep.tile([P, S + HALO], F32, name=f"acc{t}")
-            nc.scalar.activation(row[:, 0:HALO], zero[:], ACT.Silu)
-            acc.append(row)
+        acc = keep.tile([P, PACK, ROW], F32, name="acc")
+        nc.scalar.activation(acc[:, :, 0:HALO], zero[:], ACT.Silu)
 
         x_scale = keep.tile([P, S], U8, name="x_scale", align_bytes=64)
         nc.vector.tensor_copy(x_scale[:], all_scales[:].indirect(offsets[:]))
@@ -83,16 +82,13 @@ def tile_picked_dconv_silu_p_kernel(tc, x_words, x_scales, w1, w2, taps, offs, o
         w1_scale = keep.tile([P, H], U8, name="w1_scale", align_bytes=64)
         nc.vector.quantize_mx(out=w1_code[:].bitcast(FP8X4), scales=w1_scale[:], in_=w1_bf[:])
 
+        chunks, pieces = spans(CHUNK_WIDTHS), spans(PIECES)
         x_code = []
-        for first, count in spans(CHUNK_WIDTHS):
-            picked = keep.tile([P, count], U32, name=f"x_code{first}", align_bytes=64)
-            entries = offsets[:, first // LIST_ROWS : (first + count) // LIST_ROWS]
+        for j0, n in chunks:
+            picked = keep.tile([P, n], U32, name=f"x_code{j0}", align_bytes=64)
+            entries = offsets[:, j0 // LIST_ROWS : (j0 + n) // LIST_ROWS]
             nc.vector.tensor_copy(picked[:], all_words[:].bitcast(U32).indirect(entries))
-            x_code.append((first, count, picked))
-
-        def picked_words(j0, width):
-            first, picked = [(f, tile) for f, count, tile in x_code if f <= j0 < f + count][0]
-            return picked[:, j0 - first : j0 - first + width]
+            x_code.append(picked)
 
         w2_bf = keep.tile([P, PACK * N], BF16, name="w2_bf", tag="words_then_w2", align_bytes=64)
         w2_code = keep.tile([P, N], U32, name="w2_code", align_bytes=64)
@@ -111,42 +107,56 @@ def tile_picked_dconv_silu_p_kernel(tc, x_words, x_scales, w1, w2, taps, offs, o
         def tap_column(t, d):
             return tap[:, D * t + d : D * t + d + 1]
 
-        term = {}
-        for t in GPSIMD_TILES:
-            term[t] = keep.tile([P, CHUNK_WIDTHS[-1]], F32, name=f"term{t}")
-            nc.gpsimd.memset(term[t][:, 0:1], 0.0)
+        term = keep.tile([P, GPSIMD_TILES, CHUNK_WIDTHS[LAST]], F32, name="term")
+        nc.scalar.activation(term[:, :, 0:1], zero[:, 0:GPSIMD_TILES, 0:1], ACT.Silu)
 
         def on_gpsimd(c, t):
-            return c == len(CHUNKS) - 1 and t in GPSIMD_TILES
+            return c == LAST and t < GPSIMD_TILES
 
-        def first_product(c, t, h):
+        h = {}
+
+        def first_product(c, t):
             j0, n = chunks[c]
             cols = slice(t * P, (t + 1) * P)
             nc.tensor.matmul_mx(
-                out=h,
+                out=h[c, t],
                 lhsT=w1_code[:, cols].bitcast(FP8X4),
                 lhsT_scale=w1_scale[:, cols],
-                rhs=picked_words(j0, n).bitcast(FP8X4),
+                rhs=x_code[c][:].bitcast(FP8X4),
                 rhs_scale=x_scale[:, j0 : j0 + n],
                 start=True,
                 stop=True,
             )
 
-        def scalar_taps(c, t, h):
+        def taps_on_scalar(c, t):
             j0, n = chunks[c]
-            nc.scalar.activation(acc[t][:, j0 + 2 : j0 + n + 2], h, ACT.Copy, scale=tap_column(t, 2))
+            nc.scalar.activation(acc[:, t, j0 + 2 : j0 + n + 2], h[c, t], ACT.Copy, scale=tap_column(t, 2))
             if on_gpsimd(c, t):
-                nc.scalar.activation(term[t][:, 1:n], h[:, 0 : n - 1], ACT.Copy, scale=tap_column(t, 1))
+                nc.scalar.activation(term[:, t, 1:n], h[c, t][:, 0 : n - 1], ACT.Copy, scale=tap_column(t, 1))
 
-        def add_tap1(j0, n, t, h):
-            shifted = acc[t][:, j0 + 1 : j0 + n + 1]
-            nc.vector.scalar_tensor_tensor(shifted, h, tap_column(t, 1), shifted, MULT, ADD)
+        def add_terms(tiles):
+            j0, n = chunks[LAST]
+            own = acc[:, tiles, j0 : j0 + n]
+            nc.gpsimd.tensor_tensor(own, own, term[:, tiles, :], ADD)
 
-        def add_tap0(j0, n, t, h, u):
-            nc.vector.scalar_tensor_tensor(u, h, tap_column(t, 0), acc[t][:, j0 : j0 + n], MULT, ADD)
+        def add_tap1(c, j0, n):
+            a = j0 - chunks[c][0]
+            for t in range(PACK):
+                if not on_gpsimd(c, t):
+                    shifted = acc[:, t, j0 + 1 : j0 + n + 1]
+                    nc.vector.scalar_tensor_tensor(shifted, h[c, t][:, a : a + n], tap_column(t, 1), shifted, MULT, ADD)
 
-        def activate(n, u):
-            z = ring.tile([P, n * PACK], BF16, name="z", tag="z", align_bytes=64)
+        def add_tap0(c, k):
+            j0, n = pieces[k]
+            a = j0 - chunks[c][0]
+            u = ring.tile([P, PACK, n], F32, name="u", tag="u")
+            for t in sorted(range(PACK), key=lambda tile: on_gpsimd(c, tile)):
+                older = acc[:, t, j0 : j0 + n]
+                nc.vector.scalar_tensor_tensor(u[:, t, :], h[c, t][:, a : a + n], tap_column(t, 0), older, MULT, ADD)
+            return u
+
+        def activate(k, u):
+            z = ring.tile([P, PIECES[k] * PACK], BF16, name="z", tag="z", align_bytes=64)
             nc.scalar.activation(
                 z[:].rearrange("p (c i t) -> p c t i", i=LINE, t=PACK),
                 u[:].rearrange("p t (c i) -> p c t i", i=LINE),
@@ -154,7 +164,8 @@ def tile_picked_dconv_silu_p_kernel(tc, x_words, x_scales, w1, w2, taps, offs, o
             )
             return z
 
-        def quantise(n, z):
+        def quantise(k, z):
+            n = PIECES[k]
             z_code = ring.tile([P, n], U32, name="z_code", tag="z_code", align_bytes=64)
             z_scale = ring.tile([P, n], U8, name="z_scale", tag="z_scale", align_bytes=64)
             nc.vector.quantize_mx(out=z_code[:].bitcast(FP8X4), scales=z_scale[:], in_=z[:])
@@ -174,16 +185,12 @@ def tile_picked_dconv_silu_p_kernel(tc, x_words, x_scales, w1, w2, taps, offs, o
 
         out_rows = out.rearrange("(half p) s -> p half s", p=P)
 
-        def finish(k, z, copy):
-            store(k, quantise(PIECES[k], z), copy)
-
         def store(k, codes, copy):
             j0, n = pieces[k]
-            z_code, z_scale = codes
             product = psum.tile([P, 2, n], F32, name="product", tag=f"bank{k % 2}")
             for half in range(2):
-                second_product(product[:, half, :], half, z_code, z_scale)
-            result = keep.tile([P, 2, n], F32, name=f"result{j0}")
+                second_product(product[:, half, :], half, *codes)
+            result = keep.tile([P, 2, n], F32, name=f"result{k}")
             copy(result[:], product[:])
             nc.sync.dma_start(out_rows[:, :, j0 : j0 + n], result[:])
 
@@ -196,61 +203,39 @@ def tile_picked_dconv_silu_p_kernel(tc, x_words, x_scales, w1, w2, taps, offs, o
                 copy(result[:], product[:])
                 queue.dma_start(out_rows[:, half, j0 : j0 + n], result[:])
 
-        def tap1_of_chunk(c):
-            j0, n = chunks[c]
-            for t in range(PACK):
-                if on_gpsimd(c, t):
-                    own = acc[t][:, j0 : j0 + n]
-                    nc.gpsimd.tensor_tensor(own, own, term[t][:], ADD)
-                else:
-                    add_tap1(j0, n, t, h[c, t])
-
-        def tap1_of_piece(c, k):
-            j0, n = pieces[k]
-            a = j0 - chunks[c][0]
-            for t in range(PACK):
-                add_tap1(j0, n, t, h[c, t][:, a : a + n])
-
-        def tap0_of_piece(c, k):
-            j0, n = pieces[k]
-            a = j0 - chunks[c][0]
-            u = ring.tile([P, PACK, n], F32, name="u", tag="u")
-            for t in sorted(range(PACK), key=lambda t: on_gpsimd(c, t)):
-                add_tap0(j0, n, t, h[c, t][:, a : a + n], u[:, t, :])
-            return u
-
-        chunks, pieces = spans(CHUNK_WIDTHS), spans(PIECES)
-        h = {}
-        for c in range(2):
+        for c in range(LAST):
             for t in range(PACK):
                 bank = psum.tile([P, CHUNK_WIDTHS[c]], F32, name="h", tag=f"bank{PACK * c + t}")
                 h[c, t] = bank[:]
-                first_product(c, t, h[c, t])
-                scalar_taps(c, t, h[c, t])
+                first_product(c, t)
+                taps_on_scalar(c, t)
         round_w2()
-        tap1_of_chunk(0)
-        z0 = activate(PIECES[0], tap0_of_piece(0, 0))
+        add_tap1(0, *pieces[0])
+        z0 = activate(0, add_tap0(0, 0))
         for pair in ((0, 1), (2, 3)):
-            bank = psum.tile([P, 2, CHUNK_WIDTHS[2]], F32, name="h_pair", tag=f"bank{2 + pair[0] // 2}")
+            bank = psum.tile([P, 2, CHUNK_WIDTHS[LAST]], F32, name="h_pair", tag=f"bank{2 + pair[0] // 2}")
             for t in pair:
-                h[2, t] = bank[:, t % 2, :]
-                first_product(2, t, h[2, t])
+                h[LAST, t] = bank[:, t % 2, :]
+                first_product(LAST, t)
             for t in pair:
-                scalar_taps(2, t, h[2, t])
-        tap1_of_piece(1, 1)
+                taps_on_scalar(LAST, t)
+
+        add_tap1(1, *pieces[1])
         nc.vector.quantize_mx(out=w2_code[:].bitcast(FP8X4), scales=w2_scale[:], in_=w2_bf[:])
-        finish(0, z0, nc.scalar.copy)
-        z1 = activate(PIECES[1], tap0_of_piece(1, 1))
-        tap1_of_piece(1, 2)
-        z2 = activate(PIECES[2], tap0_of_piece(1, 2))
-        codes1 = quantise(PIECES[1], z1)
-        tap1_of_chunk(2)
-        z3 = activate(PIECES[3], tap0_of_piece(2, 3))
-        z4 = activate(PIECES[4], tap0_of_piece(2, 4))
-        codes2 = quantise(PIECES[2], z2)
-        codes3 = quantise(PIECES[3], z3)
-        codes4 = quantise(PIECES[4], z4)
+        store(0, quantise(0, z0), nc.scalar.copy)
+        z1 = activate(1, add_tap0(1, 1))
+        add_tap1(1, *pieces[2])
+        z2 = activate(2, add_tap0(1, 2))
+
+        add_terms(slice(0, 1))
+        add_terms(slice(1, GPSIMD_TILES))
+        add_tap1(LAST, *chunks[LAST])
+        codes1 = quantise(1, z1)
+        z3 = activate(3, add_tap0(LAST, 3))
+        z4 = activate(4, add_tap0(LAST, 4))
+
+        codes2, codes3, codes4 = quantise(2, z2), quantise(3, z3), quantise(4, z4)
         store(1, codes1, nc.vector.tensor_copy)
-        store_halves(2, codes2, 4)
+        store_halves(2, codes2, PACK)
         store(3, codes3, nc.scalar.copy)
-        store_halves(4, codes4, 6)
+        store_halves(4, codes4, PACK + 2)

@@ -22,6 +22,7 @@ QUADRANT = 32
 SCALE_ROWS = 4
 LIST_ROWS = 16
 LINE = 4
+SPREAD = P // (K // QUADRANT)
 HALO = D - 1
 ROW = S + 8
 
@@ -51,27 +52,31 @@ def tile_picked_dconv_silu_p_kernel(tc, x_words, x_scales, w1, w2, taps, offs, o
         offsets = keep.tile([P, S // LIST_ROWS], U16, name="offsets")
         nc.sync.dma_start(offsets[:], offs)
 
-        all_scales = keep.tile([P, T], U8, name="all_scales", align_bytes=64)
+        all_scales = keep.tile([P, T], U8, name="all_scales", tag="scales_then_w2", align_bytes=64)
         nc.vector.memset(all_scales[:].bitcast(I32), 0)
-        for r in range(SCALE_ROWS):
-            rows = x_scales[0, r : K // QUADRANT : SCALE_ROWS, :]
-            nc.sync.dma_start(all_scales[r:P:QUADRANT, :].bitcast(I32), rows.bitcast(I32))
+        nc.sync.dma_start(all_scales[0:P:SPREAD, :].bitcast(I32), x_scales[0].bitcast(I32))
 
         nc.sync.dma_start(w1_raw[:, 1:PACK, :], w1_rows[:, 1:PACK, :])
         all_words = keep.tile([P, T], I32, name="all_words", tag="words_then_w2", align_bytes=64)
         nc.sync.dma_start(all_words[:], x_words[0].rearrange("p n t -> p (n t)").bitcast(I32))
         tap = keep.tile([P, PACK * D], F32, name="tap")
         nc.sync.dma_start(tap[:], taps.rearrange("(p t) d -> p (t d)", t=PACK))
-        w2_raw = keep.tile([P, PACK, N], F32, name="w2_raw")
-        nc.sync.dma_start(w2_raw[:], w2.rearrange("(p j) c -> p j c", j=PACK))
 
         zero = keep.tile([P, PACK, HALO], F32, name="zero")
         nc.vector.memset(zero[:], 0.0)
         acc = keep.tile([P, PACK, ROW], F32, name="acc")
         nc.scalar.activation(acc[:, :, 0:HALO], zero[:], ACT.Silu)
 
+        picked_scales = keep.tile([P, S], U8, name="picked_scales", align_bytes=64)
+        nc.vector.tensor_copy(picked_scales[:], all_scales[:].indirect(offsets[:]))
         x_scale = keep.tile([P, S], U8, name="x_scale", align_bytes=64)
-        nc.vector.tensor_copy(x_scale[:], all_scales[:].indirect(offsets[:]))
+        nc.vector.memset(x_scale[:].bitcast(I32), 0)
+        for r in range(SCALE_ROWS):
+            nc.sync.dma_start(
+                x_scale[r:P:QUADRANT, :].bitcast(I32), picked_scales[SPREAD * r : P : QUADRANT, :].bitcast(I32)
+            )
+        w2_raw = keep.tile([P, PACK, N], F32, name="w2_raw", tag="scales_then_w2", align_bytes=64)
+        nc.sync.dma_start(w2_raw[:], w2.rearrange("(p j) c -> p j c", j=PACK))
 
         w1_bf = keep.tile([P, PACK * H], BF16, name="w1_bf", align_bytes=64)
         w1_dst = w1_bf[:].rearrange("p (t m j) -> p m j t", t=PACK, j=PACK)

@@ -54,7 +54,9 @@ def tile_picked_dconv_silu_p_kernel(tc, x_words, x_scales, w1, w2, taps, offs, o
 
         all_scales = keep.tile([P, T], U8, name="all_scales", tag="scales_then_w2", align_bytes=64)
         nc.vector.memset(all_scales[:].bitcast(I32), 0)
-        nc.sync.dma_start(all_scales[0:P:SPREAD, :].bitcast(I32), x_scales[0].bitcast(I32))
+        for a in range(2):
+            rows = x_scales[0, 8 * a : 8 * a + 8, :]
+            nc.sync.dma_start(all_scales[64 * a : 64 * a + QUADRANT : SCALE_ROWS, :].bitcast(I32), rows.bitcast(I32))
 
         nc.sync.dma_start(w1_raw[:, 1:PACK, :], w1_rows[:, 1:PACK, :])
         all_words = keep.tile([P, T], I32, name="all_words", tag="words_then_w2", align_bytes=64)
@@ -71,9 +73,11 @@ def tile_picked_dconv_silu_p_kernel(tc, x_words, x_scales, w1, w2, taps, offs, o
         nc.vector.tensor_copy(picked_scales[:], all_scales[:].indirect(offsets[:]))
         x_scale = keep.tile([P, S], U8, name="x_scale", align_bytes=64)
         nc.vector.memset(x_scale[:].bitcast(I32), 0)
-        for r in range(SCALE_ROWS):
+        for q in range(P // QUADRANT):
+            first = 64 * (q // 2) + 16 * (q % 2)
             nc.sync.dma_start(
-                x_scale[r:P:QUADRANT, :].bitcast(I32), picked_scales[SPREAD * r : P : QUADRANT, :].bitcast(I32)
+                x_scale[QUADRANT * q : QUADRANT * q + SCALE_ROWS, :].bitcast(I32),
+                picked_scales[first : first + 16 : SCALE_ROWS, :].bitcast(I32),
             )
         w2_raw = keep.tile([P, PACK, N], F32, name="w2_raw", tag="scales_then_w2", align_bytes=64)
         nc.sync.dma_start(w2_raw[:], w2.rearrange("(p j) c -> p j c", j=PACK))
@@ -192,21 +196,20 @@ def tile_picked_dconv_silu_p_kernel(tc, x_words, x_scales, w1, w2, taps, offs, o
 
         def store(k, codes, copy):
             j0, n = pieces[k]
-            product = psum.tile([P, 2, n], F32, name="product", tag=f"bank{k % 2}")
+            product = psum.tile([P, 2, n], F32, name="product", tag="bank0")
             for half in range(2):
                 second_product(product[:, half, :], half, *codes)
             result = keep.tile([P, 2, n], F32, name=f"result{k}")
             copy(result[:], product[:])
             nc.sync.dma_start(out_rows[:, :, j0 : j0 + n], result[:])
 
-        def store_halves(k, codes, first_bank):
+        def store_half(k, half, codes, bank, copy, queue):
             j0, n = pieces[k]
-            for half, copy, queue in ((0, nc.scalar.copy, nc.scalar), (1, nc.vector.tensor_copy, nc.sync)):
-                product = psum.tile([P, n], F32, name="half_product", tag=f"bank{first_bank + half}")
-                second_product(product[:], half, *codes)
-                result = keep.tile([P, n], F32, name=f"half_result{k}{half}")
-                copy(result[:], product[:])
-                queue.dma_start(out_rows[:, half, j0 : j0 + n], result[:])
+            product = psum.tile([P, n], F32, name="half_product", tag=f"bank{bank}")
+            second_product(product[:], half, *codes)
+            result = keep.tile([P, n], F32, name=f"half_result{k}{half}")
+            copy(result[:], product[:])
+            queue.dma_start(out_rows[:, half, j0 : j0 + n], result[:])
 
         for c in range(LAST):
             for t in range(PACK):
@@ -227,8 +230,9 @@ def tile_picked_dconv_silu_p_kernel(tc, x_words, x_scales, w1, w2, taps, offs, o
 
         add_tap1(1, *pieces[1])
         nc.vector.quantize_mx(out=w2_code[:].bitcast(FP8X4), scales=w2_scale[:], in_=w2_bf[:])
-        store(0, quantise(0, z0), nc.scalar.copy)
+        codes0 = quantise(0, z0)
         z1 = activate(1, add_tap0(1, 1))
+        store(0, codes0, nc.scalar.copy)
         add_tap1(1, *pieces[2])
         z2 = activate(2, add_tap0(1, 2))
 
@@ -239,8 +243,14 @@ def tile_picked_dconv_silu_p_kernel(tc, x_words, x_scales, w1, w2, taps, offs, o
         z3 = activate(3, add_tap0(LAST, 3))
         z4 = activate(4, add_tap0(LAST, 4))
 
-        codes2, codes3, codes4 = quantise(2, z2), quantise(3, z3), quantise(4, z4)
-        store(1, codes1, nc.vector.tensor_copy)
-        store_halves(2, codes2, PACK)
+        on_scalar, on_vector = (nc.scalar.copy, nc.sync), (nc.vector.tensor_copy, nc.sync)
+        store_half(1, 0, codes1, 1, *on_vector)
+        codes2 = quantise(2, z2)
+        store_half(1, 1, codes1, PACK, *on_vector)
+        codes3 = quantise(3, z3)
+        store_half(2, 0, codes2, PACK + 2, nc.scalar.copy, nc.scalar)
+        codes4 = quantise(4, z4)
+        store_half(2, 1, codes2, PACK + 3, *on_vector)
         store(3, codes3, nc.scalar.copy)
-        store_halves(4, codes4, PACK + 2)
+        store_half(4, 0, codes4, 2, nc.scalar.copy, nc.scalar)
+        store_half(4, 1, codes4, 3, *on_vector)

@@ -247,6 +247,9 @@ def tile_picked_dconv_silu_p_kernel(tc, x_words, x_scales, w1, w2, taps, offs, o
         store_half(1, 0, codes1, 1, *on_vector)
         codes2 = quantise(2, z2)
         store_half(1, 1, codes1, PACK, *on_vector)
+        warm = psum.tile([P, 2, PIECES[1]], F32, name="warm", tag=f"bank{PACK + 1}")
+        for half in range(2):
+            second_product(warm[:, half, :], half, *codes1)
         codes3 = quantise(3, z3)
         store_half(2, 0, codes2, PACK + 2, nc.scalar.copy, nc.scalar)
         codes4 = quantise(4, z4)

@@ -30,7 +30,7 @@ CHUNKS = ((256,), (256, 256), (128, 128))
 PIECES = [width for chunk in CHUNKS for width in chunk]
 CHUNK_WIDTHS = [sum(chunk) for chunk in CHUNKS]
 LAST = len(CHUNKS) - 1
-GPSIMD_TILES = 3
+TERM_CHUNKS = (1, 2)
 W1_ON_SCALAR = 64
 RING = len(PIECES)
 
@@ -116,11 +116,12 @@ def tile_picked_dconv_silu_p_kernel(tc, x_words, x_scales, w1, w2, taps, offs, o
         def tap_column(t, d):
             return tap[:, D * t + d : D * t + d + 1]
 
-        term = keep.tile([P, GPSIMD_TILES, CHUNK_WIDTHS[LAST]], F32, name="term")
-        nc.scalar.activation(term[:, :, 0:1], zero[:, 0:GPSIMD_TILES, 0:1], ACT.Silu)
+        term0 = chunks[1][0]
+        term = keep.tile([P, S - term0], F32, name="term")
+        nc.scalar.activation(term[:, 0:1], zero[:, 0, 0:1], ACT.Silu)
 
         def on_gpsimd(c, t):
-            return c == LAST and t < GPSIMD_TILES
+            return c in TERM_CHUNKS and t == 0
 
         h = {}
 
@@ -141,12 +142,14 @@ def tile_picked_dconv_silu_p_kernel(tc, x_words, x_scales, w1, w2, taps, offs, o
             j0, n = chunks[c]
             nc.scalar.activation(acc[:, t, j0 + 2 : j0 + n + 2], h[c, t], ACT.Copy, scale=tap_column(t, 2))
             if on_gpsimd(c, t):
-                nc.scalar.activation(term[:, t, 1:n], h[c, t][:, 0 : n - 1], ACT.Copy, scale=tap_column(t, 1))
+                m = min(n, S - 1 - j0)
+                a = j0 - term0 + 1
+                nc.scalar.activation(term[:, a : a + m], h[c, t][:, 0:m], ACT.Copy, scale=tap_column(t, 1))
 
-        def add_terms(tiles):
-            j0, n = chunks[LAST]
-            own = acc[:, tiles, j0 : j0 + n]
-            nc.gpsimd.tensor_tensor(own, own, term[:, tiles, :], ADD)
+        def add_terms(c):
+            j0, n = chunks[c]
+            own = acc[:, 0, j0 : j0 + n]
+            nc.gpsimd.tensor_tensor(own, own, term[:, j0 - term0 : j0 - term0 + n], ADD)
 
         def add_tap1(c, j0, n):
             a = j0 - chunks[c][0]
@@ -196,7 +199,7 @@ def tile_picked_dconv_silu_p_kernel(tc, x_words, x_scales, w1, w2, taps, offs, o
 
         def store(k, codes, copy):
             j0, n = pieces[k]
-            product = psum.tile([P, 2, n], F32, name="product", tag="bank0")
+            product = psum.tile([P, 2, n], F32, name="product", tag="bank2")
             for half in range(2):
                 second_product(product[:, half, :], half, *codes)
             result = keep.tile([P, 2, n], F32, name=f"result{k}")
@@ -212,13 +215,14 @@ def tile_picked_dconv_silu_p_kernel(tc, x_words, x_scales, w1, w2, taps, offs, o
             queue.dma_start(out_rows[:, half, j0 : j0 + n], result[:])
 
         for c in range(LAST):
-            for t in range(PACK):
+            for t in sorted(range(PACK), key=lambda tile: on_gpsimd(c, tile)):
                 bank = psum.tile([P, CHUNK_WIDTHS[c]], F32, name="h", tag=f"bank{PACK * c + t}")
                 h[c, t] = bank[:]
                 first_product(c, t)
                 taps_on_scalar(c, t)
         round_w2()
         add_tap1(0, *pieces[0])
+        add_terms(1)
         z0 = activate(0, add_tap0(0, 0))
         for pair in ((0, 1), (2, 3)):
             bank = psum.tile([P, 2, CHUNK_WIDTHS[LAST]], F32, name="h_pair", tag=f"bank{2 + pair[0] // 2}")
@@ -228,32 +232,32 @@ def tile_picked_dconv_silu_p_kernel(tc, x_words, x_scales, w1, w2, taps, offs, o
             for t in pair:
                 taps_on_scalar(LAST, t)
 
-        add_tap1(1, *pieces[1])
         nc.vector.quantize_mx(out=w2_code[:].bitcast(FP8X4), scales=w2_scale[:], in_=w2_bf[:])
-        codes0 = quantise(0, z0)
+        add_tap1(1, *chunks[1])
         z1 = activate(1, add_tap0(1, 1))
-        store(0, codes0, nc.scalar.copy)
-        add_tap1(1, *pieces[2])
         z2 = activate(2, add_tap0(1, 2))
 
-        add_terms(slice(0, 1))
-        add_terms(slice(1, GPSIMD_TILES))
+        if LAST in TERM_CHUNKS:
+            add_terms(LAST)
         add_tap1(LAST, *chunks[LAST])
+        codes0 = quantise(0, z0)
         codes1 = quantise(1, z1)
+        store_half(0, 0, codes0, PACK + 3, nc.scalar.copy, nc.sync)
         z3 = activate(3, add_tap0(LAST, 3))
         z4 = activate(4, add_tap0(LAST, 4))
 
         on_scalar, on_vector = (nc.scalar.copy, nc.sync), (nc.vector.tensor_copy, nc.sync)
-        store_half(1, 0, codes1, 1, *on_vector)
         codes2 = quantise(2, z2)
-        store_half(1, 1, codes1, PACK, *on_vector)
+        store_half(0, 1, codes0, PACK, *on_vector)
+        codes3 = quantise(3, z3)
+        codes4 = quantise(4, z4)
+        store_half(1, 0, codes1, 0, *on_vector)
+        store_half(1, 1, codes1, 1, *on_vector)
         warm = psum.tile([P, 2, PIECES[1]], F32, name="warm", tag=f"bank{PACK + 1}")
         for half in range(2):
             second_product(warm[:, half, :], half, *codes1)
-        codes3 = quantise(3, z3)
         store_half(2, 0, codes2, PACK + 2, nc.scalar.copy, nc.scalar)
-        codes4 = quantise(4, z4)
-        store_half(2, 1, codes2, PACK + 3, *on_vector)
-        store(3, codes3, nc.scalar.copy)
-        store_half(4, 0, codes4, 2, nc.scalar.copy, nc.scalar)
-        store_half(4, 1, codes4, 3, *on_vector)
+        store_half(2, 1, codes2, PACK + 3, *on_scalar)
+        store(3, codes3, nc.vector.tensor_copy)
+        store_half(4, 0, codes4, 3, nc.scalar.copy, nc.scalar)
+        store_half(4, 1, codes4, PACK, *on_vector)

@@ -23,8 +23,8 @@ SCALE_ROWS = 4
 LIST_ROWS = 16
 LINE = 4
 SPREAD = P // (K // QUADRANT)
-HALO = D - 1
-ROW = S + 8
+FRONT = 8
+ROW = FRONT + S
 
 CHUNKS = ((256,), (256, 256), (128, 128))
 PIECES = [width for chunk in CHUNKS for width in chunk]
@@ -55,8 +55,8 @@ def tile_picked_dconv_silu_p_kernel(tc, x_words, x_scales, w1, w2, taps, offs, o
         all_scales = keep.tile([P, T], U8, name="all_scales", tag="scales_then_w2", align_bytes=64)
         nc.vector.memset(all_scales[:].bitcast(I32), 0)
         for a in range(2):
-            rows = x_scales[0, 8 * a : 8 * a + 8, :]
-            nc.sync.dma_start(all_scales[64 * a : 64 * a + QUADRANT : SCALE_ROWS, :].bitcast(I32), rows.bitcast(I32))
+            eight = x_scales[0, 8 * a : 8 * a + 8, :]
+            nc.sync.dma_start(all_scales[64 * a : 64 * a + QUADRANT : SCALE_ROWS, :].bitcast(I32), eight.bitcast(I32))
 
         nc.sync.dma_start(w1_raw[:, 1:PACK, :], w1_rows[:, 1:PACK, :])
         all_words = keep.tile([P, T], I32, name="all_words", tag="words_then_w2", align_bytes=64)
@@ -64,10 +64,16 @@ def tile_picked_dconv_silu_p_kernel(tc, x_words, x_scales, w1, w2, taps, offs, o
         tap = keep.tile([P, PACK * D], F32, name="tap")
         nc.sync.dma_start(tap[:], taps.rearrange("(p t) d -> p (t d)", t=PACK))
 
-        zero = keep.tile([P, PACK, HALO], F32, name="zero")
+        zero = keep.tile([P, 2 * PACK, 1], F32, name="zero")
         nc.vector.memset(zero[:], 0.0)
-        acc = keep.tile([P, PACK, ROW], F32, name="acc")
-        nc.scalar.activation(acc[:, :, 0:HALO], zero[:], ACT.Silu)
+        rows = keep.tile([P, 2 * PACK, ROW], F32, name="rows")
+        nc.scalar.activation(rows[:, :, FRONT - 1 : FRONT], zero[:], ACT.Silu)
+
+        def far(t, j0, n):
+            return rows[:, t, FRONT + j0 : FRONT + j0 + n]
+
+        def near(t, j0, n):
+            return rows[:, PACK + t, FRONT + j0 : FRONT + j0 + n]
 
         picked_scales = keep.tile([P, S], U8, name="picked_scales", align_bytes=64)
         nc.vector.tensor_copy(picked_scales[:], all_scales[:].indirect(offsets[:]))
@@ -118,7 +124,6 @@ def tile_picked_dconv_silu_p_kernel(tc, x_words, x_scales, w1, w2, taps, offs, o
 
         term0 = chunks[1][0]
         term = keep.tile([P, S - term0], F32, name="term")
-        nc.scalar.activation(term[:, 0:1], zero[:, 0, 0:1], ACT.Silu)
 
         def on_gpsimd(c, t):
             return c in TERM_CHUNKS and t == 0
@@ -140,30 +145,29 @@ def tile_picked_dconv_silu_p_kernel(tc, x_words, x_scales, w1, w2, taps, offs, o
 
         def taps_on_scalar(c, t):
             j0, n = chunks[c]
-            nc.scalar.activation(acc[:, t, j0 + 2 : j0 + n + 2], h[c, t], ACT.Copy, scale=tap_column(t, 2))
+            m = min(n, S - 2 - j0)
+            nc.scalar.activation(far(t, j0, m), h[c, t][:, 0:m], ACT.Copy, scale=tap_column(t, 2))
             if on_gpsimd(c, t):
                 m = min(n, S - 1 - j0)
-                a = j0 - term0 + 1
-                nc.scalar.activation(term[:, a : a + m], h[c, t][:, 0:m], ACT.Copy, scale=tap_column(t, 1))
+                nc.scalar.activation(term[:, j0 - term0 : j0 - term0 + m], h[c, t][:, 0:m], ACT.Copy, scale=tap_column(t, 1))
 
         def add_terms(c):
             j0, n = chunks[c]
-            own = acc[:, 0, j0 : j0 + n]
-            nc.gpsimd.tensor_tensor(own, own, term[:, j0 - term0 : j0 - term0 + n], ADD)
+            m = min(n, S - 1 - j0)
+            nc.gpsimd.tensor_tensor(near(0, j0, m), term[:, j0 - term0 : j0 - term0 + m], far(0, j0 - 1, m), ADD)
 
         def add_tap1(c, j0, n):
-            a = j0 - chunks[c][0]
+            m = min(n, S - 1 - j0)
             for t in range(PACK):
                 if not on_gpsimd(c, t):
-                    shifted = acc[:, t, j0 + 1 : j0 + n + 1]
-                    nc.vector.scalar_tensor_tensor(shifted, h[c, t][:, a : a + n], tap_column(t, 1), shifted, MULT, ADD)
+                    nc.vector.scalar_tensor_tensor(near(t, j0, m), h[c, t][:, 0:m], tap_column(t, 1), far(t, j0 - 1, m), MULT, ADD)
 
         def add_tap0(c, k):
             j0, n = pieces[k]
             a = j0 - chunks[c][0]
             u = ring.tile([P, PACK, n], F32, name="u", tag="u")
             for t in sorted(range(PACK), key=lambda tile: on_gpsimd(c, tile)):
-                older = acc[:, t, j0 : j0 + n]
+                older = near(t, j0 - 1, n)
                 nc.vector.scalar_tensor_tensor(u[:, t, :], h[c, t][:, a : a + n], tap_column(t, 0), older, MULT, ADD)
             return u
 

@@ -22,7 +22,6 @@ QUADRANT = 32
 SCALE_ROWS = 4
 LIST_ROWS = 16
 LINE = 4
-SPREAD = P // (K // QUADRANT)
 FRONT = 8
 ROW = FRONT + S
 
@@ -30,9 +29,7 @@ CHUNKS = ((256,), (256, 256), (128, 128))
 PIECES = [width for chunk in CHUNKS for width in chunk]
 CHUNK_WIDTHS = [sum(chunk) for chunk in CHUNKS]
 LAST = len(CHUNKS) - 1
-TERM_CHUNKS = (1, 2)
 W1_ON_SCALAR = 64
-RING = len(PIECES)
 
 
 def spans(widths):
@@ -43,7 +40,6 @@ def tile_picked_dconv_silu_p_kernel(tc, x_words, x_scales, w1, w2, taps, offs, o
     nc = tc.nc
     with ExitStack() as ctx:
         keep = ctx.enter_context(tc.tile_pool(name="keep", bufs=1))
-        ring = ctx.enter_context(tc.tile_pool(name="ring", bufs=RING))
         psum = ctx.enter_context(tc.psum_pool(name="psum", bufs=1))
 
         w1_raw = keep.tile([P, PACK, H], F32, name="w1_raw")
@@ -106,8 +102,6 @@ def tile_picked_dconv_silu_p_kernel(tc, x_words, x_scales, w1, w2, taps, offs, o
             x_code.append(picked)
 
         w2_bf = keep.tile([P, PACK * N], BF16, name="w2_bf", tag="words_then_w2", align_bytes=64)
-        w2_code = keep.tile([P, N], U32, name="w2_code", align_bytes=64)
-        w2_scale = keep.tile([P, N], U8, name="w2_scale", align_bytes=64)
 
         def round_w2():
             nc.gpsimd.tensor_scalar(
@@ -122,146 +116,185 @@ def tile_picked_dconv_silu_p_kernel(tc, x_words, x_scales, w1, w2, taps, offs, o
         def tap_column(t, d):
             return tap[:, D * t + d : D * t + d + 1]
 
-        term0 = chunks[1][0]
-        term = keep.tile([P, S - term0], F32, name="term")
-
-        def on_gpsimd(c, t):
-            return c in TERM_CHUNKS and t == 0
-
         h = {}
 
-        def first_product(c, t):
+        def first_products(c, tiles, bank):
             j0, n = chunks[c]
-            cols = slice(t * P, (t + 1) * P)
-            nc.tensor.matmul_mx(
-                out=h[c, t],
-                lhsT=w1_code[:, cols].bitcast(FP8X4),
-                lhsT_scale=w1_scale[:, cols],
-                rhs=x_code[c][:].bitcast(FP8X4),
-                rhs_scale=x_scale[:, j0 : j0 + n],
-                start=True,
-                stop=True,
-            )
+            held = psum.tile([P, len(tiles), n], F32, name="h", tag=f"bank{bank}")
+            for a, t in enumerate(tiles):
+                h[c, t] = held[:, a, :]
+                cols = slice(t * P, (t + 1) * P)
+                nc.tensor.matmul_mx(
+                    out=h[c, t],
+                    lhsT=w1_code[:, cols].bitcast(FP8X4),
+                    lhsT_scale=w1_scale[:, cols],
+                    rhs=x_code[c][:].bitcast(FP8X4),
+                    rhs_scale=x_scale[:, j0 : j0 + n],
+                    start=True,
+                    stop=True,
+                )
 
-        def taps_on_scalar(c, t):
-            j0, n = chunks[c]
-            m = min(n, S - 2 - j0)
-            nc.scalar.activation(far(t, j0, m), h[c, t][:, 0:m], ACT.Copy, scale=tap_column(t, 2))
-            if on_gpsimd(c, t):
-                m = min(n, S - 1 - j0)
-                nc.scalar.activation(term[:, j0 - term0 : j0 - term0 + m], h[c, t][:, 0:m], ACT.Copy, scale=tap_column(t, 1))
-
-        def add_terms(c):
-            j0, n = chunks[c]
-            m = min(n, S - 1 - j0)
-            nc.gpsimd.tensor_tensor(near(0, j0, m), term[:, j0 - term0 : j0 - term0 + m], far(0, j0 - 1, m), ADD)
-
-        def add_tap1(c, j0, n):
-            m = min(n, S - 1 - j0)
-            for t in range(PACK):
-                if not on_gpsimd(c, t):
-                    nc.vector.scalar_tensor_tensor(near(t, j0, m), h[c, t][:, 0:m], tap_column(t, 1), far(t, j0 - 1, m), MULT, ADD)
-
-        def add_tap0(c, k):
-            j0, n = pieces[k]
+        def source(c, t, j0, n):
             a = j0 - chunks[c][0]
-            u = ring.tile([P, PACK, n], F32, name="u", tag="u")
-            for t in sorted(range(PACK), key=lambda tile: on_gpsimd(c, tile)):
-                older = near(t, j0 - 1, n)
-                nc.vector.scalar_tensor_tensor(u[:, t, :], h[c, t][:, a : a + n], tap_column(t, 0), older, MULT, ADD)
-            return u
+            return h[c, t][:, a : a + n]
 
-        def activate(k, u):
-            z = ring.tile([P, PIECES[k] * PACK], BF16, name="z", tag="z", align_bytes=64)
+        def tap2(c, t):
+            j0, n = chunks[c]
+            n = min(n, S - 2 - j0)
+            nc.scalar.activation(far(t, j0, n), source(c, t, j0, n), ACT.Copy, scale=tap_column(t, 2))
+
+        terms = keep.tile([P, 2, S], F32, name="terms", tag="terms", align_bytes=64)
+        raw = keep.tile([P, S], F32, name="raw", tag="raw_then_code", align_bytes=64)
+
+        def make_term(c, t, j0, n):
+            n = min(n, S - 1 - j0)
+            nc.scalar.activation(terms[:, t, j0 : j0 + n], source(c, t, j0, n), ACT.Copy, scale=tap_column(t, 1))
+
+        def raw_terms(c, t):
+            j0, n = chunks[c]
+            nc.scalar.copy(raw[:, j0 : j0 + n], h[c, t])
+            nc.gpsimd.tensor_scalar(far(t, j0, n), raw[:, j0 : j0 + n], tap_column(t, 2), 0.0, MULT, ADD)
+            nc.gpsimd.tensor_scalar(terms[:, t, j0 : j0 + n], raw[:, j0 : j0 + n], tap_column(t, 1), 0.0, MULT, ADD)
+
+        def add_terms(t0, t1, j0, n):
+            n = min(n, S - 1 - j0)
+            sums = rows[:, PACK + t0 : PACK + t1, FRONT + j0 : FRONT + j0 + n]
+            older = rows[:, t0:t1, FRONT + j0 - 1 : FRONT + j0 + n - 1]
+            nc.gpsimd.tensor_tensor(sums, terms[:, t0:t1, j0 : j0 + n], older, ADD)
+
+        def tap1(c, t, j0, n):
+            n = min(n, S - 1 - j0)
+            nc.vector.scalar_tensor_tensor(near(t, j0, n), source(c, t, j0, n), tap_column(t, 1), far(t, j0 - 1, n), MULT, ADD)
+
+        u = [keep.tile([P, PACK, n], F32, name=f"u{k}", tag=f"u{k}", align_bytes=64) for k, n in enumerate(PIECES)]
+        z = [keep.tile([P, PACK * n], BF16, name=f"z{k}", tag=f"z{k}", align_bytes=64) for k, n in enumerate(PIECES)]
+
+        def tap0(c, k, tiles):
+            j0, n = pieces[k]
+            for t in tiles:
+                nc.vector.scalar_tensor_tensor(u[k][:, t, :], source(c, t, j0, n), tap_column(t, 0), near(t, j0 - 1, n), MULT, ADD)
+
+        def activate(k):
             nc.scalar.activation(
-                z[:].rearrange("p (c i t) -> p c t i", i=LINE, t=PACK),
-                u[:].rearrange("p t (c i) -> p c t i", i=LINE),
+                z[k][:].rearrange("p (c i t) -> p c t i", i=LINE, t=PACK),
+                u[k][:].rearrange("p t (c i) -> p c t i", i=LINE),
                 ACT.Silu,
             )
-            return z
 
-        def quantise(k, z):
+        codes, products = {}, {}
+
+        def quantise_w2(tag="w2_code"):
+            code = keep.tile([P, N], U32, name="w2_code", tag=tag, align_bytes=64)
+            scale = keep.tile([P, N], U8, name="w2_scale", align_bytes=64)
+            nc.vector.quantize_mx(out=code[:].bitcast(FP8X4), scales=scale[:], in_=w2_bf[:])
+            codes["w2"] = code, scale
+
+        def quantise(k, tag=None):
             n = PIECES[k]
-            z_code = ring.tile([P, n], U32, name="z_code", tag="z_code", align_bytes=64)
-            z_scale = ring.tile([P, n], U8, name="z_scale", tag="z_scale", align_bytes=64)
-            nc.vector.quantize_mx(out=z_code[:].bitcast(FP8X4), scales=z_scale[:], in_=z[:])
-            return z_code, z_scale
+            code = keep.tile([P, n], U32, name=f"z_code{k}", tag=tag or f"z_code{k}", align_bytes=64)
+            scale = keep.tile([P, n], U8, name=f"z_scale{k}", align_bytes=64)
+            nc.vector.quantize_mx(out=code[:].bitcast(FP8X4), scales=scale[:], in_=z[k][:])
+            codes[k] = code, scale
 
-        def second_product(dst, half, z_code, z_scale):
+        def second_product(dst, half, k):
             cols = slice(half * P, (half + 1) * P)
             nc.tensor.matmul_mx(
                 out=dst,
-                lhsT=w2_code[:, cols].bitcast(FP8X4),
-                lhsT_scale=w2_scale[:, cols],
-                rhs=z_code[:].bitcast(FP8X4),
-                rhs_scale=z_scale[:],
+                lhsT=codes["w2"][0][:, cols].bitcast(FP8X4),
+                lhsT_scale=codes["w2"][1][:, cols],
+                rhs=codes[k][0][:].bitcast(FP8X4),
+                rhs_scale=codes[k][1][:],
                 start=True,
                 stop=True,
             )
 
         out_rows = out.rearrange("(half p) s -> p half s", p=P)
 
-        def store(k, codes, copy):
+        def multiply(k, half, bank):
+            product = psum.tile([P, PIECES[k]], F32, name="half_product", tag=f"bank{bank}")
+            second_product(product[:], half, k)
+            products[k, half] = product
+
+        def store_half(k, half, copy, queue, tag=None):
             j0, n = pieces[k]
-            product = psum.tile([P, 2, n], F32, name="product", tag="bank2")
+            result = keep.tile([P, n], F32, name=f"half_result{k}{half}", tag=tag or f"result{k}{half}", align_bytes=64)
+            copy(result[:], products[k, half][:])
+            queue.dma_start(out_rows[:, half, j0 : j0 + n], result[:])
+
+        def store_both(k, bank, copy):
+            j0, n = pieces[k]
+            product = psum.tile([P, 2, n], F32, name="product", tag=f"bank{bank}")
             for half in range(2):
-                second_product(product[:, half, :], half, *codes)
+                second_product(product[:, half, :], half, k)
             result = keep.tile([P, 2, n], F32, name=f"result{k}")
             copy(result[:], product[:])
             nc.sync.dma_start(out_rows[:, :, j0 : j0 + n], result[:])
 
-        def store_half(k, half, codes, bank, copy, queue):
-            j0, n = pieces[k]
-            product = psum.tile([P, n], F32, name="half_product", tag=f"bank{bank}")
-            second_product(product[:], half, *codes)
-            result = keep.tile([P, n], F32, name=f"half_result{k}{half}")
-            copy(result[:], product[:])
-            queue.dma_start(out_rows[:, half, j0 : j0 + n], result[:])
-
-        for c in range(LAST):
-            for t in sorted(range(PACK), key=lambda tile: on_gpsimd(c, tile)):
-                bank = psum.tile([P, CHUNK_WIDTHS[c]], F32, name="h", tag=f"bank{PACK * c + t}")
-                h[c, t] = bank[:]
-                first_product(c, t)
-                taps_on_scalar(c, t)
-        round_w2()
-        add_tap1(0, *pieces[0])
-        add_terms(1)
-        z0 = activate(0, add_tap0(0, 0))
-        for pair in ((0, 1), (2, 3)):
-            bank = psum.tile([P, 2, CHUNK_WIDTHS[LAST]], F32, name="h_pair", tag=f"bank{2 + pair[0] // 2}")
-            for t in pair:
-                h[LAST, t] = bank[:, t % 2, :]
-                first_product(LAST, t)
-            for t in pair:
-                taps_on_scalar(LAST, t)
-
-        nc.vector.quantize_mx(out=w2_code[:].bitcast(FP8X4), scales=w2_scale[:], in_=w2_bf[:])
-        add_tap1(1, *chunks[1])
-        z1 = activate(1, add_tap0(1, 1))
-        z2 = activate(2, add_tap0(1, 2))
-
-        if LAST in TERM_CHUNKS:
-            add_terms(LAST)
-        add_tap1(LAST, *chunks[LAST])
-        codes0 = quantise(0, z0)
-        codes1 = quantise(1, z1)
-        store_half(0, 0, codes0, PACK + 3, nc.scalar.copy, nc.sync)
-        z3 = activate(3, add_tap0(LAST, 3))
-        z4 = activate(4, add_tap0(LAST, 4))
+        def warm_up(bank, k):
+            warm = psum.tile([P, 2, PIECES[k]], F32, name="warm", tag=f"bank{bank}")
+            for half in range(2):
+                second_product(warm[:, half, :], half, k)
 
         on_scalar, on_vector = (nc.scalar.copy, nc.sync), (nc.vector.tensor_copy, nc.sync)
-        codes2 = quantise(2, z2)
-        store_half(0, 1, codes0, PACK, *on_vector)
-        codes3 = quantise(3, z3)
-        codes4 = quantise(4, z4)
-        store_half(1, 0, codes1, 0, *on_vector)
-        store_half(1, 1, codes1, 1, *on_vector)
-        warm = psum.tile([P, 2, PIECES[1]], F32, name="warm", tag=f"bank{PACK + 1}")
-        for half in range(2):
-            second_product(warm[:, half, :], half, *codes1)
-        store_half(2, 0, codes2, PACK + 2, nc.scalar.copy, nc.scalar)
-        store_half(2, 1, codes2, PACK + 3, *on_scalar)
-        store(3, codes3, nc.vector.tensor_copy)
-        store_half(4, 0, codes4, 3, nc.scalar.copy, nc.scalar)
-        store_half(4, 1, codes4, PACK, *on_vector)
+
+        for t in range(PACK):
+            first_products(0, (t,), t)
+            tap2(0, t)
+        for t in (0, 2, 3, 1):
+            first_products(1, (t,), PACK + t)
+            if t == 0:
+                raw_terms(1, t)
+            else:
+                tap2(1, t)
+        round_w2()
+        for t in range(PACK):
+            tap1(0, t, *chunks[0])
+        tap0(0, 0, range(PACK))
+        add_terms(0, 1, *chunks[1])
+        activate(0)
+        first_products(LAST, (0, 1), 2)
+        first_products(LAST, (2, 3), 3)
+        for t in (0, 1):
+            tap2(LAST, t)
+            make_term(LAST, t, *chunks[LAST])
+        for t in (2, 3):
+            tap2(LAST, t)
+        tap1(1, 2, *chunks[1])
+        tap1(1, 3, *chunks[1])
+        tap1(1, 1, *chunks[1])
+        tap0(1, 1, (2, 3, 1))
+        quantise_w2("raw_then_code")
+        tap0(1, 1, (0,))
+        activate(1)
+        tap0(1, 2, (2, 3, 1, 0))
+        activate(2)
+        add_terms(0, 2, *chunks[LAST])
+        tap1(LAST, 2, *chunks[LAST])
+        tap1(LAST, 3, *chunks[LAST])
+        quantise(0, "terms")
+        quantise(1)
+        multiply(0, 0, 7)
+        store_half(0, 0, *on_scalar)
+        tap0(LAST, 3, (2, 3, 1, 0))
+        activate(3)
+        tap0(LAST, 4, (2, 3, 1, 0))
+        activate(4)
+        quantise(2)
+        multiply(0, 1, 4)
+        store_half(0, 1, *on_vector)
+        quantise(3)
+        quantise(4)
+        multiply(1, 0, 0)
+        store_half(1, 0, *on_vector)
+        multiply(1, 1, 1)
+        store_half(1, 1, *on_vector)
+        warm_up(5, 1)
+        multiply(2, 0, 6)
+        store_half(2, 0, nc.scalar.copy, nc.scalar)
+        multiply(2, 1, 7)
+        store_half(2, 1, *on_scalar)
+        store_both(3, 2, nc.vector.tensor_copy)
+        multiply(4, 0, 3)
+        store_half(4, 0, nc.scalar.copy, nc.scalar)
+        multiply(4, 1, 4)
+        store_half(4, 1, *on_vector)

@@ -42,13 +42,13 @@ def tile_picked_dconv_silu_p_kernel(tc, x_words, x_scales, w1, w2, taps, offs, o
         keep = ctx.enter_context(tc.tile_pool(name="keep", bufs=1))
         psum = ctx.enter_context(tc.psum_pool(name="psum", bufs=1))
 
-        w1_raw = keep.tile([P, PACK, H], F32, name="w1_raw")
+        w1_raw = keep.tile([P, PACK, H], F32, name="w1_raw", tag="w1_then_w2", align_bytes=64)
         w1_rows = w1.rearrange("(p j) c -> p j c", j=PACK)
         nc.sync.dma_start(w1_raw[:, 0:1, :], w1_rows[:, 0:1, :])
         offsets = keep.tile([P, S // LIST_ROWS], U16, name="offsets")
         nc.sync.dma_start(offsets[:], offs)
 
-        all_scales = keep.tile([P, T], U8, name="all_scales", tag="scales_then_w2", align_bytes=64)
+        all_scales = keep.tile([P, T], U8, name="all_scales", tag="scales_then_taps", align_bytes=64)
         nc.vector.memset(all_scales[:].bitcast(I32), 0)
         for a in range(2):
             eight = x_scales[0, 8 * a : 8 * a + 8, :]
@@ -57,8 +57,6 @@ def tile_picked_dconv_silu_p_kernel(tc, x_words, x_scales, w1, w2, taps, offs, o
         nc.sync.dma_start(w1_raw[:, 1:PACK, :], w1_rows[:, 1:PACK, :])
         all_words = keep.tile([P, T], I32, name="all_words", tag="words_then_w2", align_bytes=64)
         nc.sync.dma_start(all_words[:], x_words[0].rearrange("p n t -> p (n t)").bitcast(I32))
-        tap = keep.tile([P, PACK * D], F32, name="tap")
-        nc.sync.dma_start(tap[:], taps.rearrange("(p t) d -> p (t d)", t=PACK))
 
         zero = keep.tile([P, 2 * PACK, 1], F32, name="zero")
         nc.vector.memset(zero[:], 0.0)
@@ -81,14 +79,16 @@ def tile_picked_dconv_silu_p_kernel(tc, x_words, x_scales, w1, w2, taps, offs, o
                 x_scale[QUADRANT * q : QUADRANT * q + SCALE_ROWS, :].bitcast(I32),
                 picked_scales[first : first + 16 : SCALE_ROWS, :].bitcast(I32),
             )
-        w2_raw = keep.tile([P, PACK, N], F32, name="w2_raw", tag="scales_then_w2", align_bytes=64)
-        nc.sync.dma_start(w2_raw[:], w2.rearrange("(p j) c -> p j c", j=PACK))
+        tap = keep.tile([P, PACK * D], F32, name="tap", tag="scales_then_taps", align_bytes=64)
+        nc.sync.dma_start(tap[:], taps.rearrange("(p t) d -> p (t d)", t=PACK))
 
         w1_bf = keep.tile([P, PACK * H], BF16, name="w1_bf", align_bytes=64)
         w1_dst = w1_bf[:].rearrange("p (t m j) -> p m j t", t=PACK, j=PACK)
         w1_src = w1_raw[:].rearrange("p j (m t) -> p m j t", t=PACK)
         nc.scalar.copy(w1_dst[:, 0:W1_ON_SCALAR], w1_src[:, 0:W1_ON_SCALAR])
         nc.vector.tensor_copy(w1_dst[:, W1_ON_SCALAR:P], w1_src[:, W1_ON_SCALAR:P])
+        w2_raw = keep.tile([P, PACK, N], F32, name="w2_raw", tag="w1_then_w2", align_bytes=64)
+        nc.sync.dma_start(w2_raw[:], w2.rearrange("(p j) c -> p j c", j=PACK))
         w1_code = keep.tile([P, H], U32, name="w1_code", align_bytes=64)
         w1_scale = keep.tile([P, H], U8, name="w1_scale", align_bytes=64)
         nc.vector.quantize_mx(out=w1_code[:].bitcast(FP8X4), scales=w1_scale[:], in_=w1_bf[:])

from contextlib import ExitStack

import concourse.mybir as mybir

K, T, S, D, H, N = 512, 2048, 1024, 3, 512, 256
FLOPS = 2 * K * H * S + 2 * H * N * S

F32 = mybir.dt.float32
BF16 = mybir.dt.bfloat16
I32 = mybir.dt.int32
U32 = mybir.dt.uint32
U16 = mybir.dt.uint16
U8 = mybir.dt.uint8
FP8X4 = mybir.dt.float8_e4m3fn_x4
ACT = mybir.ActivationFunctionType
MULT = mybir.AluOpType.mult
ADD = mybir.AluOpType.add

P = 128
PACK = 4
QUADRANT = 32
SCALE_ROWS = 4
LIST_ROWS = 16
LINE = 4
FRONT = 8
ROW = FRONT + S

CHUNKS = ((256,), (256, 256), (128, 128))
PIECES = [width for chunk in CHUNKS for width in chunk]
CHUNK_WIDTHS = [sum(chunk) for chunk in CHUNKS]
LAST = len(CHUNKS) - 1
W1_ON_SCALAR = 64


def spans(widths):
    return [(sum(widths[:c]), width) for c, width in enumerate(widths)]


def tile_picked_dconv_silu_p_kernel(tc, x_words, x_scales, w1, w2, taps, offs, out):
    nc = tc.nc
    with ExitStack() as ctx:
        keep = ctx.enter_context(tc.tile_pool(name="keep", bufs=1))
        psum = ctx.enter_context(tc.psum_pool(name="psum", bufs=1))

        w1_raw = keep.tile([P, PACK, H], F32, name="w1_raw", tag="w1_then_w2", align_bytes=64)
        w1_rows = w1.rearrange("(p j) c -> p j c", j=PACK)
        nc.sync.dma_start(w1_raw[:, 0:1, :], w1_rows[:, 0:1, :])
        offsets = keep.tile([P, S // LIST_ROWS], U16, name="offsets")
        nc.sync.dma_start(offsets[:], offs)

        all_scales = keep.tile([P, T], U8, name="all_scales", tag="scales_then_taps", align_bytes=64)
        nc.vector.memset(all_scales[:].bitcast(I32), 0)
        for a in range(2):
            eight = x_scales[0, 8 * a : 8 * a + 8, :]
            nc.sync.dma_start(all_scales[64 * a : 64 * a + QUADRANT : SCALE_ROWS, :].bitcast(I32), eight.bitcast(I32))

        nc.sync.dma_start(w1_raw[:, 1:PACK, :], w1_rows[:, 1:PACK, :])
        all_words = keep.tile([P, T], I32, name="all_words", tag="words_then_w2", align_bytes=64)
        nc.sync.dma_start(all_words[:], x_words[0].rearrange("p n t -> p (n t)").bitcast(I32))

        zero = keep.tile([P, 2 * PACK, 1], F32, name="zero")
        nc.vector.memset(zero[:], 0.0)
        rows = keep.tile([P, 2 * PACK, ROW], F32, name="rows")
        nc.scalar.activation(rows[:, :, FRONT - 1 : FRONT], zero[:], ACT.Silu)

        def far(t, j0, n):
            return rows[:, t, FRONT + j0 : FRONT + j0 + n]

        def near(t, j0, n):
            return rows[:, PACK + t, FRONT + j0 : FRONT + j0 + n]

        picked_scales = keep.tile([P, S], U8, name="picked_scales", align_bytes=64)
        nc.vector.tensor_copy(picked_scales[:], all_scales[:].indirect(offsets[:]))
        x_scale = keep.tile([P, S], U8, name="x_scale", align_bytes=64)
        nc.vector.memset(x_scale[:].bitcast(I32), 0)
        for q in range(P // QUADRANT):
            first = 64 * (q // 2) + 16 * (q % 2)
            nc.sync.dma_start(
                x_scale[QUADRANT * q : QUADRANT * q + SCALE_ROWS, :].bitcast(I32),
                picked_scales[first : first + 16 : SCALE_ROWS, :].bitcast(I32),
            )
        tap = keep.tile([P, PACK * D], F32, name="tap", tag="scales_then_taps", align_bytes=64)
        nc.sync.dma_start(tap[:], taps.rearrange("(p t) d -> p (t d)", t=PACK))

        w1_bf = keep.tile([P, PACK * H], BF16, name="w1_bf", align_bytes=64)
        w1_dst = w1_bf[:].rearrange("p (t m j) -> p m j t", t=PACK, j=PACK)
        w1_src = w1_raw[:].rearrange("p j (m t) -> p m j t", t=PACK)
        nc.scalar.copy(w1_dst[:, 0:W1_ON_SCALAR], w1_src[:, 0:W1_ON_SCALAR])
        nc.vector.tensor_copy(w1_dst[:, W1_ON_SCALAR:P], w1_src[:, W1_ON_SCALAR:P])
        w2_raw = keep.tile([P, PACK, N], F32, name="w2_raw", tag="w1_then_w2", align_bytes=64)
        nc.sync.dma_start(w2_raw[:], w2.rearrange("(p j) c -> p j c", j=PACK))
        w1_code = keep.tile([P, H], U32, name="w1_code", align_bytes=64)
        w1_scale = keep.tile([P, H], U8, name="w1_scale", align_bytes=64)
        nc.vector.quantize_mx(out=w1_code[:].bitcast(FP8X4), scales=w1_scale[:], in_=w1_bf[:])

        chunks, pieces = spans(CHUNK_WIDTHS), spans(PIECES)
        x_code = []
        for j0, n in chunks:
            picked = keep.tile([P, n], U32, name=f"x_code{j0}", align_bytes=64)
            entries = offsets[:, j0 // LIST_ROWS : (j0 + n) // LIST_ROWS]
            nc.vector.tensor_copy(picked[:], all_words[:].bitcast(U32).indirect(entries))
            x_code.append(picked)

        w2_bf = keep.tile([P, PACK * N], BF16, name="w2_bf", tag="words_then_w2", align_bytes=64)

        def round_w2():
            nc.gpsimd.tensor_scalar(
                w2_bf[:].rearrange("p (c j) -> p c j", j=PACK),
                w2_raw[:].rearrange("p j c -> p c j"),
                1.0,
                0.0,
                MULT,
                ADD,
            )

        def tap_column(t, d):
            return tap[:, D * t + d : D * t + d + 1]

        h = {}

        def first_products(c, tiles, bank):
            j0, n = chunks[c]
            held = psum.tile([P, len(tiles), n], F32, name="h", tag=f"bank{bank}")
            for a, t in enumerate(tiles):
                h[c, t] = held[:, a, :]
                cols = slice(t * P, (t + 1) * P)
                nc.tensor.matmul_mx(
                    out=h[c, t],
                    lhsT=w1_code[:, cols].bitcast(FP8X4),
                    lhsT_scale=w1_scale[:, cols],
                    rhs=x_code[c][:].bitcast(FP8X4),
                    rhs_scale=x_scale[:, j0 : j0 + n],
                    start=True,
                    stop=True,
                )

        def source(c, t, j0, n):
            a = j0 - chunks[c][0]
            return h[c, t][:, a : a + n]

        def tap2(c, t):
            j0, n = chunks[c]
            n = min(n, S - 2 - j0)
            nc.scalar.activation(far(t, j0, n), source(c, t, j0, n), ACT.Copy, scale=tap_column(t, 2))

        terms = keep.tile([P, 2, S], F32, name="terms", tag="terms", align_bytes=64)
        raw = keep.tile([P, S], F32, name="raw", tag="raw_then_code", align_bytes=64)

        def make_term(c, t, j0, n):
            n = min(n, S - 1 - j0)
            nc.scalar.activation(terms[:, t, j0 : j0 + n], source(c, t, j0, n), ACT.Copy, scale=tap_column(t, 1))

        def raw_terms(c, t):
            j0, n = chunks[c]
            nc.scalar.copy(raw[:, j0 : j0 + n], h[c, t])
            nc.gpsimd.tensor_scalar(far(t, j0, n), raw[:, j0 : j0 + n], tap_column(t, 2), 0.0, MULT, ADD)
            nc.gpsimd.tensor_scalar(terms[:, t, j0 : j0 + n], raw[:, j0 : j0 + n], tap_column(t, 1), 0.0, MULT, ADD)

        def add_terms(t0, t1, j0, n):
            n = min(n, S - 1 - j0)
            sums = rows[:, PACK + t0 : PACK + t1, FRONT + j0 : FRONT + j0 + n]
            older = rows[:, t0:t1, FRONT + j0 - 1 : FRONT + j0 + n - 1]
            nc.gpsimd.tensor_tensor(sums, terms[:, t0:t1, j0 : j0 + n], older, ADD)

        def tap1(c, t, j0, n):
            n = min(n, S - 1 - j0)
            nc.vector.scalar_tensor_tensor(near(t, j0, n), source(c, t, j0, n), tap_column(t, 1), far(t, j0 - 1, n), MULT, ADD)

        u = [keep.tile([P, PACK, n], F32, name=f"u{k}", tag=f"u{k}", align_bytes=64) for k, n in enumerate(PIECES)]
        z = [keep.tile([P, PACK * n], BF16, name=f"z{k}", tag=f"z{k}", align_bytes=64) for k, n in enumerate(PIECES)]

        def tap0(c, k, tiles):
            j0, n = pieces[k]
            for t in tiles:
                nc.vector.scalar_tensor_tensor(u[k][:, t, :], source(c, t, j0, n), tap_column(t, 0), near(t, j0 - 1, n), MULT, ADD)

        def activate(k):
            nc.scalar.activation(
                z[k][:].rearrange("p (c i t) -> p c t i", i=LINE, t=PACK),
                u[k][:].rearrange("p t (c i) -> p c t i", i=LINE),
                ACT.Silu,
            )

        codes, products = {}, {}

        def quantise_w2(tag="w2_code"):
            code = keep.tile([P, N], U32, name="w2_code", tag=tag, align_bytes=64)
            scale = keep.tile([P, N], U8, name="w2_scale", align_bytes=64)
            nc.vector.quantize_mx(out=code[:].bitcast(FP8X4), scales=scale[:], in_=w2_bf[:])
            codes["w2"] = code, scale

        def quantise(k, tag=None):
            n = PIECES[k]
            code = keep.tile([P, n], U32, name=f"z_code{k}", tag=tag or f"z_code{k}", align_bytes=64)
            scale = keep.tile([P, n], U8, name=f"z_scale{k}", align_bytes=64)
            nc.vector.quantize_mx(out=code[:].bitcast(FP8X4), scales=scale[:], in_=z[k][:])
            codes[k] = code, scale

        def second_product(dst, half, k):
            cols = slice(half * P, (half + 1) * P)
            nc.tensor.matmul_mx(
                out=dst,
                lhsT=codes["w2"][0][:, cols].bitcast(FP8X4),
                lhsT_scale=codes["w2"][1][:, cols],
                rhs=codes[k][0][:].bitcast(FP8X4),
                rhs_scale=codes[k][1][:],
                start=True,
                stop=True,
            )

        out_rows = out.rearrange("(half p) s -> p half s", p=P)

        def multiply(k, half, bank):
            product = psum.tile([P, PIECES[k]], F32, name="half_product", tag=f"bank{bank}")
            second_product(product[:], half, k)
            products[k, half] = product

        def store_half(k, half, copy, queue, tag=None):
            j0, n = pieces[k]
            result = keep.tile([P, n], F32, name=f"half_result{k}{half}", tag=tag or f"result{k}{half}", align_bytes=64)
            copy(result[:], products[k, half][:])
            queue.dma_start(out_rows[:, half, j0 : j0 + n], result[:])

        def store_both(k, bank, copy):
            j0, n = pieces[k]
            product = psum.tile([P, 2, n], F32, name="product", tag=f"bank{bank}")
            for half in range(2):
                second_product(product[:, half, :], half, k)
            result = keep.tile([P, 2, n], F32, name=f"result{k}")
            copy(result[:], product[:])
            nc.sync.dma_start(out_rows[:, :, j0 : j0 + n], result[:])

        def warm_up(bank, k):
            warm = psum.tile([P, 2, PIECES[k]], F32, name="warm", tag=f"bank{bank}")
            for half in range(2):
                second_product(warm[:, half, :], half, k)

        on_scalar, on_vector = (nc.scalar.copy, nc.sync), (nc.vector.tensor_copy, nc.sync)

        for t in range(PACK):
            first_products(0, (t,), t)
            tap2(0, t)
        for t in (0, 2, 3, 1):
            first_products(1, (t,), PACK + t)
            if t == 0:
                raw_terms(1, t)
            else:
                tap2(1, t)
        round_w2()
        for t in range(PACK):
            tap1(0, t, *chunks[0])
        tap0(0, 0, range(PACK))
        add_terms(0, 1, *chunks[1])
        activate(0)
        first_products(LAST, (0, 1), 2)
        first_products(LAST, (2, 3), 3)
        for t in (0, 1):
            tap2(LAST, t)
            make_term(LAST, t, *chunks[LAST])
        for t in (2, 3):
            tap2(LAST, t)
        tap1(1, 2, *chunks[1])
        tap1(1, 3, *chunks[1])
        tap1(1, 1, *chunks[1])
        tap0(1, 1, (2, 3, 1))
        quantise_w2("raw_then_code")
        tap0(1, 1, (0,))
        activate(1)
        tap0(1, 2, (2, 3, 1, 0))
        activate(2)
        add_terms(0, 2, *chunks[LAST])
        tap1(LAST, 2, *chunks[LAST])
        tap1(LAST, 3, *chunks[LAST])
        quantise(0, "terms")
        quantise(1)
        multiply(0, 0, 7)
        store_half(0, 0, *on_scalar)
        tap0(LAST, 3, (2, 3, 1, 0))
        activate(3)
        tap0(LAST, 4, (2, 3, 1, 0))
        activate(4)
        quantise(2)
        multiply(0, 1, 4)
        store_half(0, 1, *on_vector)
        quantise(3)
        quantise(4)
        multiply(1, 0, 0)
        store_half(1, 0, *on_vector)
        multiply(1, 1, 1)
        store_half(1, 1, *on_vector)
        warm_up(5, 1)
        multiply(2, 0, 6)
        store_half(2, 0, nc.scalar.copy, nc.scalar)
        multiply(2, 1, 7)
        store_half(2, 1, *on_scalar)
        store_both(3, 2, nc.vector.tensor_copy)
        multiply(4, 0, 3)
        store_half(4, 0, nc.scalar.copy, nc.scalar)
        multiply(4, 1, 4)
        store_half(4, 1, *on_vector)
